import numpy as np
import ml_dtypes


def mxq(x, axis, fmt="e4m3"):
    dtype, down = {"e4m3": (ml_dtypes.float8_e4m3fn, 7), "e5m2": (ml_dtypes.float8_e5m2, 14)}[fmt]
    v = np.moveaxis(np.asarray(x, np.float32).astype(ml_dtypes.bfloat16).astype(np.float64), axis, -1)
    blocks = v.reshape(v.shape[:-1] + (-1, 32))
    amax = np.abs(blocks).max(-1, keepdims=True)
    byte = np.maximum(np.where(amax > 0, np.frexp(amax)[1] - 1 + 127, 0) - down, 1)
    scale = np.exp2(byte - 127.0)
    codes = (blocks / scale).astype(np.float32).astype(dtype).astype(np.float64)
    return np.moveaxis((codes * scale).reshape(v.shape), -1, axis)


WIDE = False


def mx_kscale(k):
    if not WIDE:
        return np.ones(k)
    levels = np.array([10, -10, 5, -5, 0])
    if k % 512:
        return np.exp2(np.random.permutation(np.resize(levels, k // 32))).repeat(32)
    a = np.empty((k // 512, 16))
    for p in range(k // 512):
        a[p, :8] = np.random.permutation(np.resize(levels, 8))
        for g in range(8):
            far = levels[np.abs(levels - a[p, g]) >= 10]
            a[p, g + 8] = far[np.random.randint(len(far))]
    return np.exp2(a.ravel()).repeat(32)


BF16 = ml_dtypes.bfloat16


def bf(x):
    return np.asarray(x, np.float32).astype(BF16)


def f64(x):
    return np.asarray(x).astype(np.float64)


E2M1 = np.array([0.0, 0.5, 1.0, 1.5, 2.0, 3.0, 4.0, 6.0, -0.0, -0.5, -1.0, -1.5, -2.0, -3.0, -4.0, -6.0])


def pack_weight(w, fmt):
    k, n = w.shape
    w = f64(bf(w)).reshape(k // 32, 32, n)
    amax = np.abs(w).max(1)
    if fmt == "e4m3":
        byte = np.frexp(amax)[1] - 1 + 127 - 7
    else:
        mant, ex = np.frexp(amax / 6.0)
        byte = np.where(mant > 0.5, ex, ex - 1) + 127
    byte = np.clip(np.where(amax > 0, byte, 1), 1, 254)
    scaled = (w * np.exp2(127.0 - byte)[:, None, :]).reshape(k, n).astype(np.float32)
    by_word = np.ascontiguousarray(scaled.reshape(k // 512, 128, 4, n).transpose(0, 1, 3, 2))
    if fmt == "e4m3":
        words = by_word.astype(ml_dtypes.float8_e4m3fn).view(np.uint8)
    else:
        c = by_word.astype(ml_dtypes.float4_e2m1fn).view(np.uint8) & 0xF
        words = c[..., 0::2] | (c[..., 1::2] << 4)
    return np.ascontiguousarray(words), np.ascontiguousarray(byte.astype(np.uint8).reshape(k // 512, 16, n))


def unpack_weight(words, scales, fmt):
    g, p, n, _ = words.shape
    if fmt == "e4m3":
        vals = np.ascontiguousarray(words).view(ml_dtypes.float8_e4m3fn).astype(np.float64)
    else:
        nib = np.empty((g, p, n, 4), np.uint8)
        nib[..., 0::2] = words & 0xF
        nib[..., 1::2] = words >> 4
        vals = E2M1[nib]
    vals = vals * np.repeat(np.exp2(scales.astype(np.float64) - 127.0), 8, axis=1)[..., None]
    return vals.transpose(0, 1, 3, 2).reshape(g * 512, n)
def pack4(w):
    words, scales = pack_weight(w, "e2m1")
    return words.reshape(words.shape[0], 128, -1), scales


def unpack4(words, scales):
    return unpack_weight(words.reshape(words.shape[0], 128, -1, 2), scales, "e2m1")


def planes(Y):
    n, m = Y.shape
    b = f64(bf(Y)).reshape(n // 32, 32, m)
    amax = np.abs(b).max(1)
    byte = np.clip(np.where(amax > 0, np.frexp(amax)[1] - 1 + 127 - 7, 1), 1, 254)
    codes = (b * np.exp2(127.0 - byte)[:, None, :]).reshape(n, m).astype(np.float32).astype(ml_dtypes.float8_e4m3fn).view(np.uint8)
    words = codes.reshape(n // 512, 128, 4, m).transpose(0, 1, 3, 2)
    return np.ascontiguousarray(words), np.ascontiguousarray(byte.astype(np.uint8).reshape(n // 512, 16, m))


T, D, C = 2048, 512, 1024


def setup_inputs():
    s = mx_kscale(D)
    t = mx_kscale(C)
    prec = np.exp(1.5 / np.sqrt(D) * np.random.randn(D, C))
    mean = 1.2 / np.sqrt(D) * np.random.randn(D, C)
    logw = 0.5 * np.random.randn(C)
    logc = logw + 0.5 * np.log(prec).sum(axis=0) - 0.5 * (mean * mean * prec).sum(axis=0)
    gain = np.exp(0.8 * np.random.randn(D))
    frames = np.random.randn(T, D) * s
    lin = mean * prec / s[:, None]
    quad_words, quad_scales = pack4(-0.5 * (prec - 1.0) / (s * s)[:, None])
    rel = np.exp(0.3 * np.random.randn(C)) * t
    corr_words, corr_scales = pack_weight(3.0 * np.random.randn(C, D) * gain / t[:, None], "e4m3")
    unit = gain * (1.0 + 0.1 * np.random.randn(D)) / s
    offset = 0.3 * np.random.randn(D) * gain
    return {"frames": bf(frames), "lin": bf(lin), "quad_words": quad_words, "quad_scales": quad_scales,
            "logc": bf(logc), "rel": bf(rel), "corr_words": corr_words, "corr_scales": corr_scales,
            "unit": bf(unit), "offset": bf(offset)}


def reference(frames, lin, quad_words, quad_scales, logc, rel, corr_words, corr_scales, unit, offset):
    x = f64(frames)
    z = (mxq(x, 1) @ mxq(f64(lin), 0)) + (mxq(x * x, 1) @ unpack4(quad_words, quad_scales)) + f64(logc)
    e = np.exp(z - z.max(axis=1, keepdims=True))
    post = e / e.sum(axis=1, keepdims=True)
    h = post * f64(rel)
    c = mxq(h, 1) @ unpack_weight(corr_words, corr_scales, "e4m3")
    y = x * f64(unit) + c + f64(offset)
    words, scales = planes(y.T)
    return y, words, scales

@@ -1,0 +1,539 @@
+from contextlib import ExitStack
+
+import concourse.mybir as mybir
+from concourse.masks import make_identity
+
+T, D, C = 2048, 512, 1024
+FLOPS = 2 * T * D * C * 3
+
+F32 = mybir.dt.float32
+BF16 = mybir.dt.bfloat16
+I32 = mybir.dt.int32
+U32 = mybir.dt.uint32
+U8 = mybir.dt.uint8
+FP8X4 = mybir.dt.float8_e4m3fn_x4
+FP4X4 = mybir.dt.float4_e2m1fn_x4
+ALU = mybir.AluOpType
+ACT = mybir.ActivationFunctionType
+
+P = 128
+TILES = T // P
+PAIRS = TILES // 2
+BANK = 512
+PAIRED = 12
+
+
+def tile_gmm_posterior_frame_correction_k6_kernel(
+    tc, frames, lin, quad_words, quad_scales, logc, rel, corr_words, corr_scales, unit, offset, out_0, out_1, out_2
+):
+    nc = tc.nc
+    with ExitStack() as ctx:
+        keep = ctx.enter_context(tc.tile_pool(name="keep", bufs=1))
+        work = ctx.enter_context(tc.tile_pool(name="work", bufs=2))
+        psum = ctx.enter_context(tc.psum_pool(name="psum", bufs=1))
+
+        def kept(name, shape, dtype):
+            return keep.tile(shape, dtype, name=name, align_bytes=64)
+
+        def flowing(name, shape, dtype, bufs):
+            return work.tile(shape, dtype, name=name, tag=name, bufs=bufs, align_bytes=64)
+
+        def bank(tag, bufs=1):
+            return psum.tile([P, BANK], F32, name=tag, tag=tag, bufs=bufs)
+
+        ident32 = kept("ident32", [P, P], F32)
+        ident16 = kept("ident16", [P, P], BF16)
+        b_words = kept("b_words", [P, 2 * C], U8)
+        b_scales = kept("b_scales", [P, C], U8)
+        r_words = kept("r_words", [P, 2, D], U32)
+        r_scales = kept("r_scales", [P, 2, D], U8)
+        y_scales = kept("y_scales", [P, T], U8)
+        logc_cols = kept("logc_cols", [P, 2, 4], BF16)
+        rel_cols = kept("rel_cols", [P, 2, 4], BF16)
+        unit_cols = kept("unit_cols", [P, 4], BF16)
+        unit32 = kept("unit32", [P, 4], F32)
+        offset_cols = kept("offset_cols", [P, 4, 2], BF16)
+        neg_logc = kept("neg_logc", [P, C], F32)
+        rel_all = kept("rel_all", [P, C], F32)
+        unit_diag = kept("unit_diag", [P, 4, P], BF16)
+        warm = kept("warm", [P, 1], F32)
+        warm_out = kept("warm_out", [P, 1], F32)
+        x_raw = [kept("x_raw%d" % q, [P, 2 * D], BF16) for q in range(PAIRS)]
+        x_t = [kept("x_t%d" % q, [P, 2048], BF16) for q in range(PAIRS)]
+        x_codes = [kept("x_codes%d" % q, [P, 512], U32) for q in range(PAIRS)]
+        x_scales = [kept("x_scales%d" % q, [P, 512], U8) for q in range(PAIRS)]
+        a_raw = [kept("a_raw%d" % n, [P, 4, 256], BF16) for n in range(4)]
+        a_grouped = [kept("a_grouped%d" % g, [P, 512, 4], BF16) for g in range(2)]
+        a_codes = [kept("a_codes%d" % g, [P, 512], U32) for g in range(2)]
+        a_scales = [kept("a_scales%d" % g, [P, 512], U8) for g in range(2)]
+        live = {}
+
+        def load_x(q):
+            rows = frames[2 * P * q : 2 * P * (q + 1), :]
+            nc.sync.dma_start(out=x_raw[q][:].rearrange("p (h d) -> p h d", h=2), in_=rows.rearrange("(h p) d -> p h d", h=2))
+
+        def load_a(n):
+            nc.sync.dma_start(out=a_raw[n][:], in_=lin.rearrange("(p j) n -> p j n", j=4)[:, :, 256 * n : 256 * (n + 1)])
+
+        def load_cols(dst, vec):
+            nc.sync.dma_start(out=dst[:], in_=vec.rearrange("(g m k) -> m g k", g=2, k=4))
+
+        def interleave_a(n, copy):
+            g, half = divmod(n, 2)
+            copy(
+                out=a_grouped[g][:, 256 * half : 256 * (half + 1), :].rearrange("p (c i) t -> p c t i", i=4),
+                in_=a_raw[n][:].rearrange("p t (c i) -> p c t i", i=4),
+            )
+
+        def quantise(codes, scales, values):
+            nc.vector.quantize_mx(out=codes.bitcast(FP8X4), scales=scales, in_=values)
+
+        def quantise_a(g):
+            quantise(a_codes[g][:], a_scales[g][:], a_grouped[g][:].rearrange("p c t -> p (c t)"))
+
+        def spread_on_pe(cols, g, tag, bufs):
+            ps = bank(tag, bufs)
+            view = ps[:].rearrange("q (u m e) -> q u m e", u=2, e=2)
+            for k in range(4):
+                nc.tensor.matmul(
+                    out=view[:, k // 2, :, k % 2],
+                    lhsT=cols[:, g, k : k + 1].to_broadcast([P, P]),
+                    rhs=ident16[:],
+                    start=True,
+                    stop=True,
+                )
+            return ps
+
+        def spread_out(dst, g, ps, sign):
+            nc.scalar.activation(out=dst[:, BANK * g : BANK * (g + 1)], in_=ps[:], func=ACT.Copy, scale=sign)
+
+        def x_transpose(q):
+            ps = bank("xy")
+            words = x_raw[q][:].bitcast(F32).rearrange("p (h m u) -> p h u m", h=2, u=2)
+            for h in range(2):
+                for u in range(2):
+                    slot = 2 * h + u
+                    nc.tensor.transpose(ps[:, P * slot : P * (slot + 1)], words[:, h, u, :], ident32[:])
+            live["xt", q] = ps
+
+        def x_copy(q):
+            ps = live.pop(("xt", q))
+            nc.scalar.copy(
+                out=x_t[q][:, 0:1024].bitcast(F32).rearrange("p (h t u) -> p h t u", h=2, u=2),
+                in_=ps[:].rearrange("p (h u t) -> p h t u", h=2, u=2),
+            )
+
+        def x_square(q):
+            nc.scalar.activation(out=x_t[q][:, 1024:2048], in_=x_t[q][:, 0:1024], func=ACT.Square)
+
+        def x_square_on_vector(q):
+            nc.vector.tensor_tensor(out=x_t[q][:, 1024:2048], in0=x_t[q][:, 0:1024], in1=x_t[q][:, 0:1024], op=ALU.mult)
+
+        def x_quantise(q):
+            quantise(x_codes[q][:], x_scales[q][:], x_t[q][:])
+
+        def logits(i, g):
+            q, h = divmod(i, 2)
+            ps = bank("z", 2)
+            lin_cols = slice(P * h, P * (h + 1))
+            sq_cols = slice(256 + P * h, 256 + P * (h + 1))
+            nc.tensor.matmul_mx(
+                out=ps[:], lhsT=x_codes[q][:, lin_cols].bitcast(FP8X4), lhsT_scale=x_scales[q][:, lin_cols],
+                rhs=a_codes[g][:].bitcast(FP8X4), rhs_scale=a_scales[g][:], start=True, stop=False,
+            )
+            nc.tensor.matmul_mx(
+                out=ps[:], lhsT=x_codes[q][:, sq_cols].bitcast(FP8X4), lhsT_scale=x_scales[q][:, sq_cols],
+                rhs=b_words[:, 1024 * g : 1024 * (g + 1)].bitcast(FP4X4), rhs_scale=b_scales[:, 512 * g : 512 * (g + 1)],
+                start=False, stop=True,
+            )
+            live["z", i, g] = ps
+
+        def add_logc(i, g):
+            if g == 0:
+                live["nz", i] = flowing("neg_z", [P, C], F32, 3)
+            ps = live.pop(("z", i, g))
+            cols = slice(BANK * g, BANK * (g + 1))
+            nc.vector.tensor_tensor(
+                out=live["nz", i][:, cols].rearrange("p (u m e) -> p u m e", u=2, e=2),
+                in0=neg_logc[:, cols].rearrange("p (u m e) -> p u m e", u=2, e=2),
+                in1=ps[:].rearrange("p (m u e) -> p u m e", u=2, e=2),
+                op=ALU.subtract,
+            )
+
+        def row_max(i):
+            neg_max = flowing("neg_max", [P, 1], F32, 3)
+            nc.vector.tensor_reduce(out=neg_max[:], in_=live["nz", i][:], axis=mybir.AxisListType.X, op=ALU.min)
+            live["nm", i] = neg_max
+
+        def exponent(i):
+            e = flowing("e", [P, C], F32, 3)
+            total = flowing("total", [P, 1], F32, 3)
+            nc.scalar.activation(
+                out=e[:], in_=live.pop(("nz", i))[:], func=ACT.Exp, bias=live.pop(("nm", i))[:], scale=-1.0,
+                accum_out=total[:],
+            )
+            live["e", i] = e
+            live["total", i] = total
+
+        def invert(i):
+            inv = flowing("inv", [P, 1], F32, 3)
+            nc.vector.reciprocal(out=inv[:], in_=live.pop(("total", i))[:])
+            live["inv", i] = inv
+
+        def normalise(i):
+            h16 = flowing("h16", [P, C], BF16, 3)
+            nc.vector.scalar_tensor_tensor(
+                out=h16[:], in0=live.pop(("e", i))[:], scalar=live.pop(("inv", i))[:], in1=rel_all[:],
+                op0=ALU.mult, op1=ALU.mult,
+            )
+            live["h", i] = h16
+
+        def weigh(i):
+            er = flowing("weighted", [P, C], F32, 1)
+            nc.gpsimd.tensor_tensor(out=er[:], in0=live.pop(("e", i))[:], in1=rel_all[:], op=ALU.mult)
+            live["er", i] = er
+
+        def scale_rows(i):
+            h16 = flowing("h16", [P, C], BF16, 3)
+            nc.vector.tensor_scalar(
+                out=h16[:], in0=live.pop(("er", i))[:], scalar1=live.pop(("inv", i))[:], scalar2=None, op0=ALU.mult
+            )
+            live["h", i] = h16
+
+        def h_transpose(i, tag="ht", bufs=1):
+            ps = bank(tag, bufs)
+            words = live.pop(("h", i))[:].bitcast(F32)
+            for slot in range(4):
+                cols = slice(P * slot, P * (slot + 1))
+                nc.tensor.transpose(ps[:, cols], words[:, cols], ident32[:])
+            live["ht", i] = ps
+
+        def group_of(i):
+            return (i, 1) if i >= PAIRED else (i - i % 2, 2)
+
+        def h_copy(i, copy):
+            first, n = group_of(i)
+            if i == first:
+                live["hT", first] = flowing("h_t", [P, 1024 * n], BF16, 3)
+            dst = live["hT", first][:].bitcast(F32).rearrange("p (g h t u) -> p g h t u", g=2, h=n, u=2)
+            copy(out=dst[:, :, i - first, :, :], in_=live.pop(("ht", i))[:].rearrange("p (g u t) -> p g t u", g=2, u=2))
+
+        def h_quantise(first):
+            n = group_of(first)[1]
+            codes = flowing("h_codes", [P, 256 * n], U32, 3)
+            scales = flowing("h_scales", [P, 256 * n], U8, 3)
+            quantise(codes[:], scales[:], live.pop(("hT", first))[:])
+            live["hq", first] = (codes, scales)
+
+        def correction(first):
+            n = group_of(first)[1]
+            width = P * n
+            codes, scales = live.pop(("hq", first))
+            for b in range(n):
+                ps = bank("c%d" % ((first + b) % 2))
+                for kk in range(4 // n):
+                    k = (4 // n) * b + kk
+                    chans = slice(P * k, P * (k + 1))
+                    for g in range(2):
+                        toks = slice(width * g, width * (g + 1))
+                        nc.tensor.matmul_mx(
+                            out=ps[:, width * kk : width * (kk + 1)],
+                            lhsT=r_words[:, g, chans].bitcast(FP8X4), lhsT_scale=r_scales[:, g, chans],
+                            rhs=codes[:, toks].bitcast(FP8X4), rhs_scale=scales[:, toks],
+                            start=(g == 0), stop=(g == 1),
+                        )
+                live["c", first, b] = ps
+
+        def c_copy(first, b, on_vector=False):
+            n = group_of(first)[1]
+            width = P * n
+            chunks = 4 // n
+            if b == 0:
+                live["cT", first] = flowing("c_t", [P, 4, width], F32, 4)
+            ps = live.pop(("c", first, b))
+            dst = live["cT", first]
+            if on_vector:
+                ks = slice(chunks * b, chunks * (b + 1))
+                nc.vector.tensor_tensor(
+                    out=dst[:, ks, :], in0=ps[:].rearrange("p (k t) -> p k t", k=chunks),
+                    in1=offset_cols[:, ks, 0:1].to_broadcast([P, chunks, width]), op=ALU.add,
+                )
+            else:
+                for kk in range(chunks):
+                    k = chunks * b + kk
+                    nc.scalar.activation(
+                        out=dst[:, k, :], in_=ps[:, width * kk : width * (kk + 1)], func=ACT.Identity,
+                        bias=offset_cols[:, k, 0:1],
+                    )
+
+        def y_scaled(i, tag="y"):
+            q, h = divmod(i, 2)
+            ps = bank(tag, 2)
+            xv = x_t[q][:, 0:1024].rearrange("p (h t j) -> p h j t", h=2, j=4)
+            yv = ps[:].rearrange("t (m j) -> t j m", j=4)
+            for j in range(4):
+                nc.tensor.matmul(out=yv[:, j, :], lhsT=xv[:, h, j, :], rhs=unit_diag[:, j, :], start=(j == 0), stop=False)
+            live["y", i] = ps
+
+        def y_sum(i):
+            first = group_of(i)[0]
+            h = i - first
+            ps = live["y", i]
+            c_t = live["cT", first]
+            for k in range(4):
+                nc.tensor.matmul(
+                    out=ps[:, P * k : P * (k + 1)], lhsT=c_t[:, k, P * h : P * (h + 1)], rhs=ident32[:],
+                    is_transpose=True, start=False, stop=(k == 3),
+                )
+
+        def y_copy(i, copy):
+            y32 = flowing("y32", [P, D], F32, 6)
+            copy(out=y32[:], in_=live["y", i][:])
+            nc.sync.dma_start(out=out_0[P * i : P * (i + 1), :], in_=y32[:])
+            live["y32", i] = y32
+
+        def y_round(i, copy, source):
+            y16 = flowing("y16", [P, D], BF16, 6)
+            copy(
+                out=y16[:].rearrange("p (u m e) -> p u m e", u=2, e=2),
+                in_=live[source, i][:].rearrange("p (m u e) -> p u m e", u=2, e=2),
+            )
+            live["y16", i] = y16
+
+        def y_transpose(tiles, tag="xy"):
+            ps = bank(tag)
+            for n, i in enumerate(tiles):
+                words = live.pop(("y16", i))[:].bitcast(F32)
+                for u in range(2):
+                    slot = 2 * n + u
+                    nc.tensor.transpose(ps[:, P * slot : P * (slot + 1)], words[:, P * u : P * (u + 1)], ident32[:])
+            live["yt", tiles[0]] = ps
+
+        def yt_copy(tiles, copy):
+            first, n = tiles[0], len(tiles)
+            q, h = divmod(first, 2)
+            if ("yT", q) not in live:
+                live["yT", q] = flowing("y_t", [P, 1024], BF16, 3)
+            dst = live["yT", q][:, 512 * h : 512 * (h + n)]
+            copy(
+                out=dst.bitcast(F32).rearrange("p (h t u) -> p h t u", h=n, u=2),
+                in_=live.pop(("yt", first))[:, 0 : 256 * n].rearrange("p (h u t) -> p h t u", h=n, u=2),
+            )
+
+        def y_quantise(q):
+            codes = flowing("y_codes", [P, 256], U32, 4)
+            toks = slice(256 * q, 256 * (q + 1))
+            quantise(codes[:], y_scales[:, toks], live.pop(("yT", q))[:])
+            words = out_1[0].rearrange("p m t -> p (m t)").bitcast(I32)
+            nc.sync.dma_start(out=words[:, toks], in_=codes[:].bitcast(I32))
+
+        def store_scales(lo, hi, queues):
+            for quad in range(4):
+                queues[quad % len(queues)].dma_start(
+                    out=out_2[0, 4 * quad : 4 * quad + 4, lo:hi].bitcast(I32),
+                    in_=y_scales[32 * quad : 32 * quad + 4, lo:hi].bitcast(I32),
+                )
+
+        on_s = nc.scalar.copy
+        on_v = nc.vector.tensor_copy
+
+        nc.vector.memset(warm[:], 0.0)
+        nc.vector.memset(b_scales[:].bitcast(I32), 0)
+        nc.vector.memset(r_scales[:].rearrange("p g n -> p (g n)").bitcast(I32), 0)
+        nc.scalar.activation(out=warm_out[:], in_=warm[:], func=ACT.Exp)
+        make_identity(nc, ident32[:])
+        make_identity(nc, ident16[:])
+        load_x(0)
+        load_a(0)
+        load_cols(logc_cols, logc)
+        load_a(1)
+        nc.sync.dma_start(out=b_words[:].bitcast(I32), in_=quad_words[0].bitcast(I32))
+        for quad in range(4):
+            nc.sync.dma_start(
+                out=b_scales[32 * quad : 32 * quad + 4, :].bitcast(I32),
+                in_=quad_scales[0, 4 * quad : 4 * quad + 4, :].bitcast(I32),
+            )
+        load_a(2)
+        load_a(3)
+        load_x(1)
+        load_x(2)
+        load_cols(rel_cols, rel)
+        nc.sync.dma_start(out=unit_cols[:], in_=unit.rearrange("(p j) -> p j", j=4))
+        load_x(3)
+        nc.sync.dma_start(
+            out=r_words[:].bitcast(I32), in_=corr_words.rearrange("g p n t -> p g (n t)").bitcast(I32)
+        )
+        for quad in range(4):
+            nc.sync.dma_start(
+                out=r_scales[32 * quad : 32 * quad + 4, :, :].bitcast(I32),
+                in_=corr_scales[:, 4 * quad : 4 * quad + 4, :].rearrange("g r n -> r g n").bitcast(I32),
+            )
+        with nc.allow_non_contiguous_dma(reason="one bias value a partition"):
+            nc.sync.dma_start(out=offset_cols[:, :, 0], in_=offset.rearrange("(k p) -> p k", p=P))
+        for q in range(4, PAIRS):
+            load_x(q)
+
+        with tc.manual_schedule(engines={mybir.EngineType.DVE, mybir.EngineType.Pool}):
+            x_transpose(0)
+            x_copy(0)
+            interleave_a(0, on_v)
+            spread0 = spread_on_pe(logc_cols, 0, "c0", 1)
+            spread1 = spread_on_pe(logc_cols, 1, "c1", 1)
+            interleave_a(1, on_v)
+            spread_out(neg_logc, 0, spread0, -1.0)
+            x_square_on_vector(0)
+            quantise_a(0)
+            x_quantise(0)
+            spread_out(neg_logc, 1, spread1, -1.0)
+            interleave_a(2, on_s)
+            interleave_a(3, on_v)
+            logits(0, 0)
+            logits(1, 0)
+            x_transpose(1)
+            add_logc(0, 0)
+            quantise_a(1)
+            x_copy(1)
+            x_square(1)
+            add_logc(1, 0)
+            logits(0, 1)
+            logits(1, 1)
+            add_logc(0, 1)
+            spread0 = spread_on_pe(rel_cols, 0, "c0", 1)
+            spread1 = spread_on_pe(rel_cols, 1, "c1", 1)
+            x_quantise(1)
+            spread_out(rel_all, 0, spread0, 1.0)
+            spread_out(rel_all, 1, spread1, 1.0)
+
+            LAST_WEIGHED = -1
+
+            def pair_ok(first):
+                return 0 <= first < PAIRED
+
+            def finish_rows(i):
+                if i <= LAST_WEIGHED:
+                    scale_rows(i)
+                else:
+                    normalise(i)
+
+            for s in range(1, TILES):
+                odd = s % 2 == 1
+                q_x = 2 if s == 1 else (s // 2 + 2 if not odd and s // 2 + 2 < PAIRS else None)
+                if 0 <= s - 2 <= LAST_WEIGHED:
+                    weigh(s - 2)
+                if odd and pair_ok(s - 7):
+                    y_transpose([s - 7, s - 6])
+                if s >= 3:
+                    h_transpose(s - 3)
+                if q_x is not None:
+                    x_transpose(q_x)
+                row_max(s - 1)
+                if odd and pair_ok(s - 5):
+                    c_copy(s - 5, 0)
+                if not odd and pair_ok(s - 6):
+                    y_copy(s - 5, on_s)
+                if s >= 3:
+                    h_copy(s - 3, on_s)
+                exponent(s - 1)
+                if not odd and pair_ok(s - 4):
+                    y_scaled(s - 4)
+                if odd and pair_ok(s - 5):
+                    y_scaled(s - 4)
+                if s >= 2:
+                    add_logc(s, 0)
+                add_logc(s, 1)
+                if s + 1 < TILES:
+                    logits(s + 1, 0)
+                    logits(s + 1, 1)
+                if s >= 2:
+                    invert(s - 2)
+                if s == 1:
+                    nc.scalar.copy(out=unit32[:], in_=unit_cols[:])
+                    for j in range(4):
+                        nc.scalar.activation(out=unit_diag[:, j, :], in_=ident16[:], func=ACT.Copy, scale=unit32[:, j : j + 1])
+                if odd:
+                    if pair_ok(s - 5):
+                        c_copy(s - 5, 1)
+                        y_sum(s - 5)
+                        y_sum(s - 4)
+                    if pair_ok(s - 7):
+                        yt_copy([s - 7, s - 6], on_s)
+                    if pair_ok(s - 5):
+                        y_copy(s - 5, on_s)
+                    if pair_ok(s - 9):
+                        y_quantise((s - 9) // 2)
+                    if s - 3 == PAIRED:
+                        h_quantise(s - 3)
+                        correction(s - 3)
+                    if 3 <= (s + 3) // 2 < PAIRS:
+                        x_quantise((s + 3) // 2)
+                else:
+                    if s == 2:
+                        x_quantise(2)
+                    if pair_ok(s - 4):
+                        h_quantise(s - 4)
+                        correction(s - 4)
+                    if pair_ok(s - 6):
+                        y_round(s - 6, on_s, "y32")
+                        y_round(s - 5, on_s, "y32")
+                if q_x is not None:
+                    x_copy(q_x)
+                    x_square(q_x)
+                if s >= 2:
+                    finish_rows(s - 2)
+
+            e = PAIRED - 2
+            a, b, c, d = PAIRED, PAIRED + 1, PAIRED + 2, PAIRED + 3
+            row_max(d)
+        exponent(d)
+        h_transpose(b)
+        h_copy(b, on_s)
+        invert(c)
+        c_copy(a, 0, True)
+        normalise(c)
+        y_scaled(a, "z")
+        y_sum(a)
+        h_quantise(b)
+        correction(b)
+        invert(d)
+        normalise(d)
+        h_transpose(c)
+        h_copy(c, on_s)
+        h_transpose(d, "xy")
+        h_copy(d, on_s)
+        h_quantise(c)
+        c_copy(b, 0)
+        correction(c)
+        h_quantise(d)
+        correction(d)
+        y_copy(e + 1, on_s)
+        y_scaled(b, "z")
+        y_sum(b)
+        y_scaled(c)
+        y_scaled(d)
+        c_copy(c, 0, True)
+        c_copy(d, 0, True)
+        y_sum(c)
+        y_sum(d)
+        y_round(d, on_s, "y")
+        y_round(c, on_v, "y")
+        y_copy(a, on_s)
+        y_round(e, on_v, "y32")
+        y_round(e + 1, on_v, "y32")
+        y_transpose([e, e + 1])
+        y_quantise(e // 2 - 1)
+        y_copy(b, on_s)
+        y_round(a, on_v, "y32")
+        y_round(b, on_v, "y32")
+        yt_copy([e, e + 1], on_s)
+        y_quantise(e // 2)
+        y_transpose([a, b], "c0")
+        y_transpose([c], "ht")
+        y_transpose([d], "c1")
+        yt_copy([a, b], on_v)
+        yt_copy([c], on_v)
+        yt_copy([d], on_v)
+        y_copy(c, on_s)
+        y_copy(d, on_s)
+        y_quantise(a // 2)
+        y_quantise(c // 2)
+        store_scales(0, T, [nc.scalar, nc.sync])

@@ -20,7 +20,7 @@ P = 128
 TILES = T // P
 PAIRS = TILES // 2
 BANK = 512
-PAIRED = 12
+PAIRED = 0
 
 
 def tile_gmm_posterior_frame_correction_k6_kernel(
@@ -31,6 +31,8 @@ def tile_gmm_posterior_frame_correction_k6_kernel(
         keep = ctx.enter_context(tc.tile_pool(name="keep", bufs=1))
         work = ctx.enter_context(tc.tile_pool(name="work", bufs=2))
         psum = ctx.enter_context(tc.psum_pool(name="psum", bufs=1))
+
+        ctx.enter_context(tc.manual_schedule())
 
         def kept(name, shape, dtype):
             return keep.tile(shape, dtype, name=name, align_bytes=64)
@@ -56,6 +58,7 @@ def tile_gmm_posterior_frame_correction_k6_kernel(
         neg_logc = kept("neg_logc", [P, C], F32)
         rel_all = kept("rel_all", [P, C], F32)
         unit_diag = kept("unit_diag", [P, 4, P], BF16)
+        zeros = kept("zeros", [P, BANK], BF16)
         warm = kept("warm", [P, 1], F32)
         warm_out = kept("warm_out", [P, 1], F32)
         x_raw = [kept("x_raw%d" % q, [P, 2 * D], BF16) for q in range(PAIRS)]
@@ -75,8 +78,8 @@ def tile_gmm_posterior_frame_correction_k6_kernel(
         def load_a(n):
             nc.sync.dma_start(out=a_raw[n][:], in_=lin.rearrange("(p j) n -> p j n", j=4)[:, :, 256 * n : 256 * (n + 1)])
 
-        def load_cols(dst, vec):
-            nc.sync.dma_start(out=dst[:], in_=vec.rearrange("(g m k) -> m g k", g=2, k=4))
+        def load_cols(dst, vec, queue):
+            queue.dma_start(out=dst[:], in_=vec.rearrange("(g m k) -> m g k", g=2, k=4))
 
         def interleave_a(n, copy):
             g, half = divmod(n, 2)
@@ -338,14 +341,16 @@ def tile_gmm_posterior_frame_correction_k6_kernel(
         on_v = nc.vector.tensor_copy
 
         nc.vector.memset(warm[:], 0.0)
+        nc.vector.memset(zeros[:].bitcast(I32), 0)
         nc.vector.memset(b_scales[:].bitcast(I32), 0)
         nc.vector.memset(r_scales[:].rearrange("p g n -> p (g n)").bitcast(I32), 0)
         nc.scalar.activation(out=warm_out[:], in_=warm[:], func=ACT.Exp)
         make_identity(nc, ident32[:])
         make_identity(nc, ident16[:])
+        load_cols(rel_cols, rel, nc.gpsimd)
         load_x(0)
+        load_cols(logc_cols, logc, nc.sync)
         load_a(0)
-        load_cols(logc_cols, logc)
         load_a(1)
         nc.sync.dma_start(out=b_words[:].bitcast(I32), in_=quad_words[0].bitcast(I32))
         for quad in range(4):
@@ -357,9 +362,9 @@ def tile_gmm_posterior_frame_correction_k6_kernel(
         load_a(3)
         load_x(1)
         load_x(2)
-        load_cols(rel_cols, rel)
         nc.sync.dma_start(out=unit_cols[:], in_=unit.rearrange("(p j) -> p j", j=4))
         load_x(3)
+        load_x(4)
         nc.sync.dma_start(
             out=r_words[:].bitcast(I32), in_=corr_words.rearrange("g p n t -> p g (n t)").bitcast(I32)
         )
@@ -370,170 +375,170 @@ def tile_gmm_posterior_frame_correction_k6_kernel(
             )
         with nc.allow_non_contiguous_dma(reason="one bias value a partition"):
             nc.sync.dma_start(out=offset_cols[:, :, 0], in_=offset.rearrange("(k p) -> p k", p=P))
-        for q in range(4, PAIRS):
+        for q in range(5, PAIRS):
             load_x(q)
 
-        with tc.manual_schedule(engines={mybir.EngineType.DVE, mybir.EngineType.Pool}):
-            x_transpose(0)
-            x_copy(0)
-            interleave_a(0, on_v)
-            spread0 = spread_on_pe(logc_cols, 0, "c0", 1)
-            spread1 = spread_on_pe(logc_cols, 1, "c1", 1)
-            interleave_a(1, on_v)
-            spread_out(neg_logc, 0, spread0, -1.0)
-            x_square_on_vector(0)
-            quantise_a(0)
-            x_quantise(0)
-            spread_out(neg_logc, 1, spread1, -1.0)
-            interleave_a(2, on_s)
-            interleave_a(3, on_v)
-            logits(0, 0)
-            logits(1, 0)
-            x_transpose(1)
-            add_logc(0, 0)
-            quantise_a(1)
-            x_copy(1)
-            x_square(1)
-            add_logc(1, 0)
-            logits(0, 1)
-            logits(1, 1)
-            add_logc(0, 1)
-            spread0 = spread_on_pe(rel_cols, 0, "c0", 1)
-            spread1 = spread_on_pe(rel_cols, 1, "c1", 1)
-            x_quantise(1)
-            spread_out(rel_all, 0, spread0, 1.0)
-            spread_out(rel_all, 1, spread1, 1.0)
+        for n in range(4):
+            nc.tensor.matmul(out=bank("ht")[:], lhsT=zeros[:, 0:P], rhs=zeros[:], start=True, stop=True)
+        x_transpose(0)
+        x_copy(0)
+        interleave_a(0, on_v)
+        spread0 = spread_on_pe(logc_cols, 0, "c0", 1)
+        spread1 = spread_on_pe(logc_cols, 1, "c1", 1)
+        rel0 = spread_on_pe(rel_cols, 0, "y", 2)
+        rel1 = spread_on_pe(rel_cols, 1, "y", 2)
+        interleave_a(1, on_v)
+        spread_out(neg_logc, 0, spread0, -1.0)
+        x_square_on_vector(0)
+        quantise_a(0)
+        x_quantise(0)
+        spread_out(neg_logc, 1, spread1, -1.0)
+        interleave_a(2, on_s)
+        interleave_a(3, on_v)
+        logits(0, 0)
+        x_transpose(1)
+        logits(1, 0)
+        x_copy(1)
+        quantise_a(1)
+        add_logc(0, 0)
+        x_square(1)
+        logits(0, 1)
+        x_transpose(2)
+        add_logc(1, 0)
+        logits(1, 1)
+        x_copy(2)
+        add_logc(0, 1)
+        x_quantise(1)
+        x_square(2)
+        spread_out(rel_all, 0, rel0, 1.0)
+        spread_out(rel_all, 1, rel1, 1.0)
 
-            LAST_WEIGHED = -1
+        LAST_WEIGHED = -1
+        SQUARE_ON_VECTOR = (4, 6, 7)
+        ROUND_ON_VECTOR = ()
+        x_step = {1: 3, 2: 4, 4: 5, 7: 6, 9: 7}
 
-            def pair_ok(first):
-                return 0 <= first < PAIRED
+        def pair_ok(first):
+            return 0 <= first < PAIRED
 
-            def finish_rows(i):
-                if i <= LAST_WEIGHED:
-                    scale_rows(i)
-                else:
-                    normalise(i)
+        def finish_rows(i):
+            if i <= LAST_WEIGHED:
+                scale_rows(i)
+            else:
+                normalise(i)
 
-            for s in range(1, TILES):
-                odd = s % 2 == 1
-                q_x = 2 if s == 1 else (s // 2 + 2 if not odd and s // 2 + 2 < PAIRS else None)
-                if 0 <= s - 2 <= LAST_WEIGHED:
-                    weigh(s - 2)
-                if odd and pair_ok(s - 7):
-                    y_transpose([s - 7, s - 6])
-                if s >= 3:
-                    h_transpose(s - 3)
-                if q_x is not None:
-                    x_transpose(q_x)
+        def has(i):
+            return 0 <= i < TILES
+
+        for s in range(1, TILES):
+            odd = s % 2 == 1
+            late = s >= 99
+            q_x = x_step.get(s)
+            if 0 <= s - 2 <= LAST_WEIGHED:
+                weigh(s - 2)
+            if has(s - 3):
+                h_transpose(s - 3)
+            if not odd and has(s - 6):
+                y_transpose([s - 6, s - 5])
+            if s >= 2:
+                logits(s, 1)
+            if q_x is not None:
+                x_transpose(q_x)
+            if has(s - 1):
                 row_max(s - 1)
-                if odd and pair_ok(s - 5):
-                    c_copy(s - 5, 0)
-                if not odd and pair_ok(s - 6):
-                    y_copy(s - 5, on_s)
-                if s >= 3:
-                    h_copy(s - 3, on_s)
+            if has(s - 4):
+                c_copy(s - 4, 0, late)
+                y_sum(s - 4)
+            if has(s - 3):
+                h_copy(s - 3, on_s)
+            if has(s - 1):
                 exponent(s - 1)
-                if not odd and pair_ok(s - 4):
-                    y_scaled(s - 4)
-                if odd and pair_ok(s - 5):
-                    y_scaled(s - 4)
+            if has(s - 3):
+                y_scaled(s - 3)
+            if has(s):
                 if s >= 2:
                     add_logc(s, 0)
                 add_logc(s, 1)
-                if s + 1 < TILES:
-                    logits(s + 1, 0)
-                    logits(s + 1, 1)
-                if s >= 2:
-                    invert(s - 2)
-                if s == 1:
-                    nc.scalar.copy(out=unit32[:], in_=unit_cols[:])
-                    for j in range(4):
-                        nc.scalar.activation(out=unit_diag[:, j, :], in_=ident16[:], func=ACT.Copy, scale=unit32[:, j : j + 1])
-                if odd:
-                    if pair_ok(s - 5):
-                        c_copy(s - 5, 1)
-                        y_sum(s - 5)
-                        y_sum(s - 4)
-                    if pair_ok(s - 7):
-                        yt_copy([s - 7, s - 6], on_s)
-                    if pair_ok(s - 5):
-                        y_copy(s - 5, on_s)
-                    if pair_ok(s - 9):
-                        y_quantise((s - 9) // 2)
-                    if s - 3 == PAIRED:
-                        h_quantise(s - 3)
-                        correction(s - 3)
-                    if 3 <= (s + 3) // 2 < PAIRS:
-                        x_quantise((s + 3) // 2)
-                else:
-                    if s == 2:
-                        x_quantise(2)
-                    if pair_ok(s - 4):
-                        h_quantise(s - 4)
-                        correction(s - 4)
-                    if pair_ok(s - 6):
-                        y_round(s - 6, on_s, "y32")
-                        y_round(s - 5, on_s, "y32")
-                if q_x is not None:
-                    x_copy(q_x)
+            if has(s + 1):
+                logits(s + 1, 0)
+            else:
+                y_scaled(s - 1, "z")
+                y_scaled(s, "z")
+            if has(s - 2):
+                invert(s - 2)
+            if s == 1:
+                nc.scalar.copy(out=unit32[:], in_=unit_cols[:])
+                for j in range(4):
+                    nc.scalar.activation(out=unit_diag[:, j, :], in_=ident16[:], func=ACT.Copy, scale=unit32[:, j : j + 1])
+            if has(s - 3):
+                h_quantise(s - 3)
+                correction(s - 3)
+            if has(s - 4):
+                y_copy(s - 4, on_s)
+                if s - 4 not in ROUND_ON_VECTOR:
+                    y_round(s - 4, on_s, "y")
+            if not odd and has(s - 6):
+                yt_copy([s - 6, s - 5], on_v if late else on_s)
+            if odd and has(s - 7):
+                y_quantise((s - 7) // 2)
+            if not odd and s // 2 + 1 < PAIRS:
+                x_quantise(s // 2 + 1)
+            if odd and (s + 3) // 2 in SQUARE_ON_VECTOR:
+                x_square_on_vector((s + 3) // 2)
+            if q_x is not None:
+                x_copy(q_x)
+                if q_x not in SQUARE_ON_VECTOR:
                     x_square(q_x)
-                if s >= 2:
-                    finish_rows(s - 2)
+            if s - 4 in ROUND_ON_VECTOR:
+                y_round(s - 4, on_v, "y32")
+            if has(s - 2):
+                finish_rows(s - 2)
 
-            e = PAIRED - 2
-            a, b, c, d = PAIRED, PAIRED + 1, PAIRED + 2, PAIRED + 3
-            row_max(d)
-        exponent(d)
+        a, b, c, d = TILES - 4, TILES - 3, TILES - 2, TILES - 1
         h_transpose(b)
+        y_transpose([a - 2, a - 1])
+        row_max(d)
+        c_copy(a, 0)
+        exponent(d)
         h_copy(b, on_s)
         invert(c)
-        c_copy(a, 0, True)
-        normalise(c)
-        y_scaled(a, "z")
         y_sum(a)
+        y_scaled(b)
+        finish_rows(c)
+        h_transpose(c)
+        invert(d)
         h_quantise(b)
         correction(b)
-        invert(d)
-        normalise(d)
-        h_transpose(c)
         h_copy(c, on_s)
-        h_transpose(d, "xy")
-        h_copy(d, on_s)
-        h_quantise(c)
-        c_copy(b, 0)
-        correction(c)
-        h_quantise(d)
-        correction(d)
-        y_copy(e + 1, on_s)
-        y_scaled(b, "z")
-        y_sum(b)
-        y_scaled(c)
-        y_scaled(d)
-        c_copy(c, 0, True)
-        c_copy(d, 0, True)
-        y_sum(c)
-        y_sum(d)
-        y_round(d, on_s, "y")
-        y_round(c, on_v, "y")
+        normalise(d)
         y_copy(a, on_s)
-        y_round(e, on_v, "y32")
-        y_round(e + 1, on_v, "y32")
-        y_transpose([e, e + 1])
-        y_quantise(e // 2 - 1)
+        h_transpose(d)
+        h_quantise(c)
+        correction(c)
+        h_copy(d, on_s)
+        c_copy(b, 0, True)
+        y_sum(b)
+        yt_copy([a - 2, a - 1], on_s)
+        h_quantise(d)
+        c_copy(c, 0, True)
+        correction(d)
         y_copy(b, on_s)
+        y_sum(c)
         y_round(a, on_v, "y32")
+        y_quantise(a // 2 - 1)
+        c_copy(d, 0, True)
+        y_round(c, on_s, "y")
+        y_sum(d)
         y_round(b, on_v, "y32")
-        yt_copy([e, e + 1], on_s)
-        y_quantise(e // 2)
-        y_transpose([a, b], "c0")
         y_transpose([c], "ht")
-        y_transpose([d], "c1")
-        yt_copy([a, b], on_v)
+        y_transpose([a, b])
+        y_round(d, on_s, "y")
         yt_copy([c], on_v)
-        yt_copy([d], on_v)
+        y_transpose([d], "c0")
         y_copy(c, on_s)
+        yt_copy([a, b], on_v)
         y_copy(d, on_s)
+        yt_copy([d], on_v)
         y_quantise(a // 2)
         y_quantise(c // 2)
         store_scales(0, T, [nc.scalar, nc.sync])

@@ -17,10 +17,13 @@ ALU = mybir.AluOpType
 ACT = mybir.ActivationFunctionType
 
 P = 128
+PACK = 4
+BANK = 512
 TILES = T // P
 PAIRS = TILES // 2
-BANK = 512
-PAIRED = 0
+A_PART = 256
+GPSIMD_COLS = 704
+FIRST_PAIR_SQUARED_ON_VECTOR = 5
 
 
 def tile_gmm_posterior_frame_correction_k6_kernel(
@@ -31,7 +34,6 @@ def tile_gmm_posterior_frame_correction_k6_kernel(
         keep = ctx.enter_context(tc.tile_pool(name="keep", bufs=1))
         work = ctx.enter_context(tc.tile_pool(name="work", bufs=2))
         psum = ctx.enter_context(tc.psum_pool(name="psum", bufs=1))
-
         ctx.enter_context(tc.manual_schedule())
 
         def kept(name, shape, dtype):
@@ -40,8 +42,10 @@ def tile_gmm_posterior_frame_correction_k6_kernel(
         def flowing(name, shape, dtype, bufs):
             return work.tile(shape, dtype, name=name, tag=name, bufs=bufs, align_bytes=64)
 
-        def bank(tag, bufs=1):
-            return psum.tile([P, BANK], F32, name=tag, tag=tag, bufs=bufs)
+        banks = {"logits": 2, "h_turned": 1, "corr0": 1, "corr1": 1, "y": 2, "xy_turned": 1}
+
+        def bank(tag):
+            return psum.tile([P, BANK], F32, name=tag, tag=tag, bufs=banks[tag])
 
         ident32 = kept("ident32", [P, P], F32)
         ident16 = kept("ident16", [P, P], BF16)
@@ -50,132 +54,139 @@ def tile_gmm_posterior_frame_correction_k6_kernel(
         r_words = kept("r_words", [P, 2, D], U32)
         r_scales = kept("r_scales", [P, 2, D], U8)
         y_scales = kept("y_scales", [P, T], U8)
-        logc_cols = kept("logc_cols", [P, 2, 4], BF16)
-        rel_cols = kept("rel_cols", [P, 2, 4], BF16)
-        unit_cols = kept("unit_cols", [P, 4], BF16)
-        unit32 = kept("unit32", [P, 4], F32)
+        logc_cols = kept("logc_cols", [P, 2, PACK], BF16)
+        rel_cols = kept("rel_cols", [P, 2, PACK], BF16)
+        unit_cols = kept("unit_cols", [P, PACK], BF16)
+        unit32 = kept("unit32", [P, PACK], F32)
         offset_cols = kept("offset_cols", [P, 4, 2], BF16)
         neg_logc = kept("neg_logc", [P, C], F32)
         rel_all = kept("rel_all", [P, C], F32)
-        unit_diag = kept("unit_diag", [P, 4, P], BF16)
-        zeros = kept("zeros", [P, BANK], BF16)
-        warm = kept("warm", [P, 1], F32)
-        warm_out = kept("warm_out", [P, 1], F32)
+        unit_diag = kept("unit_diag", [P, PACK, P], BF16)
+        table_in = kept("table_in", [P, 1], F32)
+        table_out = kept("table_out", [P, 1], F32)
         x_raw = [kept("x_raw%d" % q, [P, 2 * D], BF16) for q in range(PAIRS)]
-        x_t = [kept("x_t%d" % q, [P, 2048], BF16) for q in range(PAIRS)]
-        x_codes = [kept("x_codes%d" % q, [P, 512], U32) for q in range(PAIRS)]
-        x_scales = [kept("x_scales%d" % q, [P, 512], U8) for q in range(PAIRS)]
-        a_raw = [kept("a_raw%d" % n, [P, 4, 256], BF16) for n in range(4)]
-        a_grouped = [kept("a_grouped%d" % g, [P, 512, 4], BF16) for g in range(2)]
-        a_codes = [kept("a_codes%d" % g, [P, 512], U32) for g in range(2)]
-        a_scales = [kept("a_scales%d" % g, [P, 512], U8) for g in range(2)]
+        x_t = [kept("x_t%d" % q, [P, 4 * D], BF16) for q in range(PAIRS)]
+        x_codes = [kept("x_codes%d" % q, [P, D], U32) for q in range(PAIRS)]
+        x_scales = [kept("x_scales%d" % q, [P, D], U8) for q in range(PAIRS)]
+        a_raw = [kept("a_raw%d" % n, [P, PACK, A_PART], BF16) for n in range(C // A_PART)]
+        a_grouped = [kept("a_grouped%d" % g, [P, BANK, PACK], BF16) for g in range(2)]
+        a_codes = [kept("a_codes%d" % g, [P, BANK], U32) for g in range(2)]
+        a_scales = [kept("a_scales%d" % g, [P, BANK], U8) for g in range(2)]
         live = {}
 
-        def load_x(q):
-            rows = frames[2 * P * q : 2 * P * (q + 1), :]
-            nc.sync.dma_start(out=x_raw[q][:].rearrange("p (h d) -> p h d", h=2), in_=rows.rearrange("(h p) d -> p h d", h=2))
+        on_scalar = nc.scalar.copy
+        on_vector = nc.vector.tensor_copy
 
-        def load_a(n):
-            nc.sync.dma_start(out=a_raw[n][:], in_=lin.rearrange("(p j) n -> p j n", j=4)[:, :, 256 * n : 256 * (n + 1)])
+        def sorted_view(ap):
+            return ap.rearrange("p (u m e) -> p u m e", u=2, e=2)
 
-        def load_cols(dst, vec, queue):
-            queue.dma_start(out=dst[:], in_=vec.rearrange("(g m k) -> m g k", g=2, k=4))
-
-        def interleave_a(n, copy):
-            g, half = divmod(n, 2)
-            copy(
-                out=a_grouped[g][:, 256 * half : 256 * (half + 1), :].rearrange("p (c i) t -> p c t i", i=4),
-                in_=a_raw[n][:].rearrange("p t (c i) -> p c t i", i=4),
-            )
+        def natural_as_sorted(ap):
+            return ap.rearrange("p (m u e) -> p u m e", u=2, e=2)
 
         def quantise(codes, scales, values):
             nc.vector.quantize_mx(out=codes.bitcast(FP8X4), scales=scales, in_=values)
 
+
+        def load_x(q):
+            rows = frames[2 * P * q : 2 * P * (q + 1), :]
+            nc.sync.dma_start(
+                out=x_raw[q][:].rearrange("p (h d) -> p h d", h=2), in_=rows.rearrange("(h p) d -> p h d", h=2)
+            )
+
+        def load_a(n):
+            rows = lin.rearrange("(p t) c -> p t c", t=PACK)
+            nc.sync.dma_start(out=a_raw[n][:], in_=rows[:, :, A_PART * n : A_PART * (n + 1)])
+
+        def load_cols(cols, vec):
+            nc.sync.dma_start(out=cols[:], in_=vec.rearrange("(g m t) -> m g t", g=2, t=PACK))
+
+        def interleave_a(n, copy):
+            g, half = divmod(n, 2)
+            copy(
+                out=a_grouped[g][:, A_PART * half : A_PART * (half + 1), :].rearrange("p (c i) t -> p c t i", i=4),
+                in_=a_raw[n][:].rearrange("p t (c i) -> p c t i", i=4),
+            )
+
         def quantise_a(g):
             quantise(a_codes[g][:], a_scales[g][:], a_grouped[g][:].rearrange("p c t -> p (c t)"))
 
-        def spread_on_pe(cols, g, tag, bufs):
-            ps = bank(tag, bufs)
-            view = ps[:].rearrange("q (u m e) -> q u m e", u=2, e=2)
-            for k in range(4):
+        def spread(cols, g, tag):
+            ps = bank(tag)
+            for t in range(PACK):
                 nc.tensor.matmul(
-                    out=view[:, k // 2, :, k % 2],
-                    lhsT=cols[:, g, k : k + 1].to_broadcast([P, P]),
-                    rhs=ident16[:],
-                    start=True,
-                    stop=True,
+                    out=sorted_view(ps[:])[:, t // 2, :, t % 2], lhsT=cols[:, g, t : t + 1].to_broadcast([P, P]),
+                    rhs=ident16[:], start=True, stop=True,
                 )
             return ps
 
         def spread_out(dst, g, ps, sign):
             nc.scalar.activation(out=dst[:, BANK * g : BANK * (g + 1)], in_=ps[:], func=ACT.Copy, scale=sign)
 
+
         def x_transpose(q):
-            ps = bank("xy")
+            ps = bank("xy_turned")
             words = x_raw[q][:].bitcast(F32).rearrange("p (h m u) -> p h u m", h=2, u=2)
             for h in range(2):
                 for u in range(2):
                     slot = 2 * h + u
                     nc.tensor.transpose(ps[:, P * slot : P * (slot + 1)], words[:, h, u, :], ident32[:])
-            live["xt", q] = ps
+            live["x_turned", q] = ps
 
         def x_copy(q):
-            ps = live.pop(("xt", q))
             nc.scalar.copy(
-                out=x_t[q][:, 0:1024].bitcast(F32).rearrange("p (h t u) -> p h t u", h=2, u=2),
-                in_=ps[:].rearrange("p (h u t) -> p h t u", h=2, u=2),
+                out=x_t[q][:, 0 : 2 * D].bitcast(F32).rearrange("p (h f u) -> p h f u", h=2, u=2),
+                in_=live.pop(("x_turned", q))[:].rearrange("p (h u f) -> p h f u", h=2, u=2),
             )
 
-        def x_square(q):
-            nc.scalar.activation(out=x_t[q][:, 1024:2048], in_=x_t[q][:, 0:1024], func=ACT.Square)
+        def x_square_on_scalar(q):
+            nc.scalar.activation(out=x_t[q][:, 2 * D : 4 * D], in_=x_t[q][:, 0 : 2 * D], func=ACT.Square)
 
         def x_square_on_vector(q):
-            nc.vector.tensor_tensor(out=x_t[q][:, 1024:2048], in0=x_t[q][:, 0:1024], in1=x_t[q][:, 0:1024], op=ALU.mult)
+            x = x_t[q][:, 0 : 2 * D]
+            nc.vector.tensor_tensor(out=x_t[q][:, 2 * D : 4 * D], in0=x, in1=x, op=ALU.mult)
 
         def x_quantise(q):
             quantise(x_codes[q][:], x_scales[q][:], x_t[q][:])
 
+
         def logits(i, g):
             q, h = divmod(i, 2)
-            ps = bank("z", 2)
-            lin_cols = slice(P * h, P * (h + 1))
-            sq_cols = slice(256 + P * h, 256 + P * (h + 1))
+            ps = bank("logits")
+            plain = slice(P * h, P * (h + 1))
+            squared = slice(2 * P + P * h, 2 * P + P * (h + 1))
             nc.tensor.matmul_mx(
-                out=ps[:], lhsT=x_codes[q][:, lin_cols].bitcast(FP8X4), lhsT_scale=x_scales[q][:, lin_cols],
+                out=ps[:], lhsT=x_codes[q][:, plain].bitcast(FP8X4), lhsT_scale=x_scales[q][:, plain],
                 rhs=a_codes[g][:].bitcast(FP8X4), rhs_scale=a_scales[g][:], start=True, stop=False,
             )
             nc.tensor.matmul_mx(
-                out=ps[:], lhsT=x_codes[q][:, sq_cols].bitcast(FP8X4), lhsT_scale=x_scales[q][:, sq_cols],
-                rhs=b_words[:, 1024 * g : 1024 * (g + 1)].bitcast(FP4X4), rhs_scale=b_scales[:, 512 * g : 512 * (g + 1)],
-                start=False, stop=True,
+                out=ps[:], lhsT=x_codes[q][:, squared].bitcast(FP8X4), lhsT_scale=x_scales[q][:, squared],
+                rhs=b_words[:, 2 * BANK * g : 2 * BANK * (g + 1)].bitcast(FP4X4),
+                rhs_scale=b_scales[:, BANK * g : BANK * (g + 1)], start=False, stop=True,
             )
             live["z", i, g] = ps
 
         def add_logc(i, g):
             if g == 0:
-                live["nz", i] = flowing("neg_z", [P, C], F32, 3)
-            ps = live.pop(("z", i, g))
+                live["neg_z", i] = flowing("neg_z", [P, C], F32, 3)
             cols = slice(BANK * g, BANK * (g + 1))
             nc.vector.tensor_tensor(
-                out=live["nz", i][:, cols].rearrange("p (u m e) -> p u m e", u=2, e=2),
-                in0=neg_logc[:, cols].rearrange("p (u m e) -> p u m e", u=2, e=2),
-                in1=ps[:].rearrange("p (m u e) -> p u m e", u=2, e=2),
-                op=ALU.subtract,
+                out=sorted_view(live["neg_z", i][:, cols]), in0=sorted_view(neg_logc[:, cols]),
+                in1=natural_as_sorted(live.pop(("z", i, g))[:]), op=ALU.subtract,
             )
 
         def row_max(i):
             neg_max = flowing("neg_max", [P, 1], F32, 3)
-            nc.vector.tensor_reduce(out=neg_max[:], in_=live["nz", i][:], axis=mybir.AxisListType.X, op=ALU.min)
-            live["nm", i] = neg_max
+            nc.vector.tensor_reduce(out=neg_max[:], in_=live["neg_z", i][:], axis=mybir.AxisListType.X, op=ALU.min)
+            live["neg_max", i] = neg_max
 
         def exponent(i):
-            e = flowing("e", [P, C], F32, 3)
+            exps = flowing("exps", [P, C], F32, 3)
             total = flowing("total", [P, 1], F32, 3)
             nc.scalar.activation(
-                out=e[:], in_=live.pop(("nz", i))[:], func=ACT.Exp, bias=live.pop(("nm", i))[:], scale=-1.0,
+                out=exps[:], in_=live.pop(("neg_z", i))[:], func=ACT.Exp, bias=live.pop(("neg_max", i))[:], scale=-1.0,
                 accum_out=total[:],
             )
-            live["e", i] = e
+            live["exps", i] = exps
             live["total", i] = total
 
         def invert(i):
@@ -183,173 +194,145 @@ def tile_gmm_posterior_frame_correction_k6_kernel(
             nc.vector.reciprocal(out=inv[:], in_=live.pop(("total", i))[:])
             live["inv", i] = inv
 
-        def normalise(i):
+        def weigh(i):
+            weighted = flowing("weighted", [P, GPSIMD_COLS], F32, 1)
+            nc.gpsimd.tensor_tensor(
+                out=weighted[:], in0=live["exps", i][:, 0:GPSIMD_COLS], in1=rel_all[:, 0:GPSIMD_COLS], op=ALU.mult
+            )
+            live["weighted", i] = weighted
+
+        def normalise(i, weighed):
             h16 = flowing("h16", [P, C], BF16, 3)
+            inv = live.pop(("inv", i))
             nc.vector.scalar_tensor_tensor(
-                out=h16[:], in0=live.pop(("e", i))[:], scalar=live.pop(("inv", i))[:], in1=rel_all[:],
+                out=h16[:, weighed:C], in0=live.pop(("exps", i))[:, weighed:C], scalar=inv[:], in1=rel_all[:, weighed:C],
                 op0=ALU.mult, op1=ALU.mult,
             )
-            live["h", i] = h16
+            if weighed:
+                nc.vector.tensor_scalar(
+                    out=h16[:, 0:weighed], in0=live.pop(("weighted", i))[:], scalar1=inv[:], scalar2=None, op0=ALU.mult
+                )
+            live["h16", i] = h16
 
-        def weigh(i):
-            er = flowing("weighted", [P, C], F32, 1)
-            nc.gpsimd.tensor_tensor(out=er[:], in0=live.pop(("e", i))[:], in1=rel_all[:], op=ALU.mult)
-            live["er", i] = er
 
-        def scale_rows(i):
-            h16 = flowing("h16", [P, C], BF16, 3)
-            nc.vector.tensor_scalar(
-                out=h16[:], in0=live.pop(("er", i))[:], scalar1=live.pop(("inv", i))[:], scalar2=None, op0=ALU.mult
-            )
-            live["h", i] = h16
-
-        def h_transpose(i, tag="ht", bufs=1):
-            ps = bank(tag, bufs)
-            words = live.pop(("h", i))[:].bitcast(F32)
+        def h_transpose(i):
+            ps = bank("h_turned")
+            words = live.pop(("h16", i))[:].bitcast(F32)
             for slot in range(4):
                 cols = slice(P * slot, P * (slot + 1))
                 nc.tensor.transpose(ps[:, cols], words[:, cols], ident32[:])
-            live["ht", i] = ps
+            live["h_turned", i] = ps
 
-        def group_of(i):
-            return (i, 1) if i >= PAIRED else (i - i % 2, 2)
+        def h_copy(i):
+            h_t = flowing("h_t", [P, C], BF16, 3)
+            nc.scalar.copy(
+                out=h_t[:].bitcast(F32).rearrange("p (g f u) -> p g f u", g=2, u=2),
+                in_=live.pop(("h_turned", i))[:].rearrange("p (g u f) -> p g f u", g=2, u=2),
+            )
+            live["h_t", i] = h_t
 
-        def h_copy(i, copy):
-            first, n = group_of(i)
-            if i == first:
-                live["hT", first] = flowing("h_t", [P, 1024 * n], BF16, 3)
-            dst = live["hT", first][:].bitcast(F32).rearrange("p (g h t u) -> p g h t u", g=2, h=n, u=2)
-            copy(out=dst[:, :, i - first, :, :], in_=live.pop(("ht", i))[:].rearrange("p (g u t) -> p g t u", g=2, u=2))
+        def h_quantise(i):
+            codes = flowing("h_codes", [P, 2 * P], U32, 3)
+            scales = flowing("h_scales", [P, 2 * P], U8, 3)
+            quantise(codes[:], scales[:], live.pop(("h_t", i))[:])
+            live["h_mx", i] = (codes, scales)
 
-        def h_quantise(first):
-            n = group_of(first)[1]
-            codes = flowing("h_codes", [P, 256 * n], U32, 3)
-            scales = flowing("h_scales", [P, 256 * n], U8, 3)
-            quantise(codes[:], scales[:], live.pop(("hT", first))[:])
-            live["hq", first] = (codes, scales)
-
-        def correction(first):
-            n = group_of(first)[1]
-            width = P * n
-            codes, scales = live.pop(("hq", first))
-            for b in range(n):
-                ps = bank("c%d" % ((first + b) % 2))
-                for kk in range(4 // n):
-                    k = (4 // n) * b + kk
-                    chans = slice(P * k, P * (k + 1))
-                    for g in range(2):
-                        toks = slice(width * g, width * (g + 1))
-                        nc.tensor.matmul_mx(
-                            out=ps[:, width * kk : width * (kk + 1)],
-                            lhsT=r_words[:, g, chans].bitcast(FP8X4), lhsT_scale=r_scales[:, g, chans],
-                            rhs=codes[:, toks].bitcast(FP8X4), rhs_scale=scales[:, toks],
-                            start=(g == 0), stop=(g == 1),
-                        )
-                live["c", first, b] = ps
-
-        def c_copy(first, b, on_vector=False):
-            n = group_of(first)[1]
-            width = P * n
-            chunks = 4 // n
-            if b == 0:
-                live["cT", first] = flowing("c_t", [P, 4, width], F32, 4)
-            ps = live.pop(("c", first, b))
-            dst = live["cT", first]
-            if on_vector:
-                ks = slice(chunks * b, chunks * (b + 1))
-                nc.vector.tensor_tensor(
-                    out=dst[:, ks, :], in0=ps[:].rearrange("p (k t) -> p k t", k=chunks),
-                    in1=offset_cols[:, ks, 0:1].to_broadcast([P, chunks, width]), op=ALU.add,
-                )
-            else:
-                for kk in range(chunks):
-                    k = chunks * b + kk
-                    nc.scalar.activation(
-                        out=dst[:, k, :], in_=ps[:, width * kk : width * (kk + 1)], func=ACT.Identity,
-                        bias=offset_cols[:, k, 0:1],
+        def correction(i):
+            codes, scales = live.pop(("h_mx", i))
+            ps = bank("corr%d" % (i % 2))
+            for k in range(4):
+                chunk = slice(P * k, P * (k + 1))
+                for g in range(2):
+                    half = slice(P * g, P * (g + 1))
+                    nc.tensor.matmul_mx(
+                        out=ps[:, chunk], lhsT=r_words[:, g, chunk].bitcast(FP8X4), lhsT_scale=r_scales[:, g, chunk],
+                        rhs=codes[:, half].bitcast(FP8X4), rhs_scale=scales[:, half], start=(g == 0), stop=(g == 1),
                     )
+            live["corr", i] = ps
 
-        def y_scaled(i, tag="y"):
+        def add_offset_on_scalar(i):
+            c_t = flowing("c_t", [P, 4, P], F32, 4)
+            ps = live.pop(("corr", i))
+            for k in range(4):
+                nc.scalar.activation(
+                    out=c_t[:, k, :], in_=ps[:, P * k : P * (k + 1)], func=ACT.Identity, bias=offset_cols[:, k, 0:1]
+                )
+            live["c_t", i] = c_t
+
+        def add_offset_on_vector(i):
+            c_t = flowing("c_t", [P, 4, P], F32, 4)
+            nc.vector.tensor_tensor(
+                out=c_t[:], in0=live.pop(("corr", i))[:].rearrange("p (k f) -> p k f", k=4),
+                in1=offset_cols[:, :, 0:1].to_broadcast([P, 4, P]), op=ALU.add,
+            )
+            live["c_t", i] = c_t
+
+        def y_scaled(i, tag):
             q, h = divmod(i, 2)
-            ps = bank(tag, 2)
-            xv = x_t[q][:, 0:1024].rearrange("p (h t j) -> p h j t", h=2, j=4)
-            yv = ps[:].rearrange("t (m j) -> t j m", j=4)
-            for j in range(4):
-                nc.tensor.matmul(out=yv[:, j, :], lhsT=xv[:, h, j, :], rhs=unit_diag[:, j, :], start=(j == 0), stop=False)
+            ps = bank(tag)
+            x_slots = x_t[q][:, 0 : 2 * D].rearrange("p (h f t) -> p h t f", h=2, t=PACK)
+            y_slots = ps[:].rearrange("f (m t) -> f t m", t=PACK)
+            for t in range(PACK):
+                nc.tensor.matmul(
+                    out=y_slots[:, t, :], lhsT=x_slots[:, h, t, :], rhs=unit_diag[:, t, :], start=(t == 0), stop=False
+                )
             live["y", i] = ps
 
         def y_sum(i):
-            first = group_of(i)[0]
-            h = i - first
-            ps = live["y", i]
-            c_t = live["cT", first]
+            c_t = live.pop(("c_t", i))
             for k in range(4):
                 nc.tensor.matmul(
-                    out=ps[:, P * k : P * (k + 1)], lhsT=c_t[:, k, P * h : P * (h + 1)], rhs=ident32[:],
+                    out=live["y", i][:, P * k : P * (k + 1)], lhsT=c_t[:, k, :], rhs=ident32[:],
                     is_transpose=True, start=False, stop=(k == 3),
                 )
 
-        def y_copy(i, copy):
+        def y_store(i):
             y32 = flowing("y32", [P, D], F32, 6)
-            copy(out=y32[:], in_=live["y", i][:])
+            nc.scalar.copy(out=y32[:], in_=live["y", i][:])
             nc.sync.dma_start(out=out_0[P * i : P * (i + 1), :], in_=y32[:])
             live["y32", i] = y32
 
         def y_round(i, copy, source):
             y16 = flowing("y16", [P, D], BF16, 6)
-            copy(
-                out=y16[:].rearrange("p (u m e) -> p u m e", u=2, e=2),
-                in_=live[source, i][:].rearrange("p (m u e) -> p u m e", u=2, e=2),
-            )
+            copy(out=sorted_view(y16[:]), in_=natural_as_sorted(live[source, i][:]))
             live["y16", i] = y16
 
-        def y_transpose(tiles, tag="xy"):
+        def y_transpose(tiles, tag):
             ps = bank(tag)
             for n, i in enumerate(tiles):
                 words = live.pop(("y16", i))[:].bitcast(F32)
                 for u in range(2):
                     slot = 2 * n + u
                     nc.tensor.transpose(ps[:, P * slot : P * (slot + 1)], words[:, P * u : P * (u + 1)], ident32[:])
-            live["yt", tiles[0]] = ps
+            live["y_turned", tiles[0]] = ps
 
-        def yt_copy(tiles, copy):
-            first, n = tiles[0], len(tiles)
-            q, h = divmod(first, 2)
-            if ("yT", q) not in live:
-                live["yT", q] = flowing("y_t", [P, 1024], BF16, 3)
-            dst = live["yT", q][:, 512 * h : 512 * (h + n)]
+        def y_turned_copy(tiles, copy):
+            q, h = divmod(tiles[0], 2)
+            n = len(tiles)
+            if h == 0:
+                live["y_t", q] = flowing("y_t", [P, 2 * D], BF16, 3)
             copy(
-                out=dst.bitcast(F32).rearrange("p (h t u) -> p h t u", h=n, u=2),
-                in_=live.pop(("yt", first))[:, 0 : 256 * n].rearrange("p (h u t) -> p h t u", h=n, u=2),
+                out=live["y_t", q][:, D * h : D * (h + n)].bitcast(F32).rearrange("p (h f u) -> p h f u", h=n, u=2),
+                in_=live.pop(("y_turned", tiles[0]))[:, 0 : 2 * P * n].rearrange("p (h u f) -> p h f u", h=n, u=2),
             )
 
         def y_quantise(q):
-            codes = flowing("y_codes", [P, 256], U32, 4)
-            toks = slice(256 * q, 256 * (q + 1))
-            quantise(codes[:], y_scales[:, toks], live.pop(("yT", q))[:])
+            codes = flowing("y_codes", [P, 2 * P], U32, 4)
+            pair_frames = slice(2 * P * q, 2 * P * (q + 1))
+            quantise(codes[:], y_scales[:, pair_frames], live.pop(("y_t", q))[:])
             words = out_1[0].rearrange("p m t -> p (m t)").bitcast(I32)
-            nc.sync.dma_start(out=words[:, toks], in_=codes[:].bitcast(I32))
+            nc.sync.dma_start(out=words[:, pair_frames], in_=codes[:].bitcast(I32))
 
-        def store_scales(lo, hi, queues):
-            for quad in range(4):
-                queues[quad % len(queues)].dma_start(
-                    out=out_2[0, 4 * quad : 4 * quad + 4, lo:hi].bitcast(I32),
-                    in_=y_scales[32 * quad : 32 * quad + 4, lo:hi].bitcast(I32),
-                )
-
-        on_s = nc.scalar.copy
-        on_v = nc.vector.tensor_copy
-
-        nc.vector.memset(warm[:], 0.0)
-        nc.vector.memset(zeros[:].bitcast(I32), 0)
+        nc.vector.memset(table_in[:], 0.0)
         nc.vector.memset(b_scales[:].bitcast(I32), 0)
         nc.vector.memset(r_scales[:].rearrange("p g n -> p (g n)").bitcast(I32), 0)
-        nc.scalar.activation(out=warm_out[:], in_=warm[:], func=ACT.Exp)
+        nc.scalar.activation(out=table_out[:], in_=table_in[:], func=ACT.Exp)
         make_identity(nc, ident32[:])
         make_identity(nc, ident16[:])
-        load_cols(rel_cols, rel, nc.gpsimd)
+
         load_x(0)
-        load_cols(logc_cols, logc, nc.sync)
+        load_cols(logc_cols, logc)
+        load_cols(rel_cols, rel)
         load_a(0)
         load_a(1)
         nc.sync.dma_start(out=b_words[:].bitcast(I32), in_=quad_words[0].bitcast(I32))
@@ -362,183 +345,164 @@ def tile_gmm_posterior_frame_correction_k6_kernel(
         load_a(3)
         load_x(1)
         load_x(2)
-        nc.sync.dma_start(out=unit_cols[:], in_=unit.rearrange("(p j) -> p j", j=4))
+        nc.sync.dma_start(out=unit_cols[:], in_=unit.rearrange("(m t) -> m t", t=PACK))
         load_x(3)
         load_x(4)
-        nc.sync.dma_start(
-            out=r_words[:].bitcast(I32), in_=corr_words.rearrange("g p n t -> p g (n t)").bitcast(I32)
-        )
+        nc.sync.dma_start(out=r_words[:].bitcast(I32), in_=corr_words.rearrange("g p n t -> p g (n t)").bitcast(I32))
         for quad in range(4):
             nc.sync.dma_start(
                 out=r_scales[32 * quad : 32 * quad + 4, :, :].bitcast(I32),
                 in_=corr_scales[:, 4 * quad : 4 * quad + 4, :].rearrange("g r n -> r g n").bitcast(I32),
             )
-        with nc.allow_non_contiguous_dma(reason="one bias value a partition"):
+        with nc.allow_non_contiguous_dma(reason="one offset a partition for each chunk of 128 channels"):
             nc.sync.dma_start(out=offset_cols[:, :, 0], in_=offset.rearrange("(k p) -> p k", p=P))
         for q in range(5, PAIRS):
             load_x(q)
 
-        for n in range(4):
-            nc.tensor.matmul(out=bank("ht")[:], lhsT=zeros[:, 0:P], rhs=zeros[:], start=True, stop=True)
         x_transpose(0)
         x_copy(0)
-        interleave_a(0, on_v)
-        spread0 = spread_on_pe(logc_cols, 0, "c0", 1)
-        spread1 = spread_on_pe(logc_cols, 1, "c1", 1)
-        rel0 = spread_on_pe(rel_cols, 0, "y", 2)
-        rel1 = spread_on_pe(rel_cols, 1, "y", 2)
-        interleave_a(1, on_v)
-        spread_out(neg_logc, 0, spread0, -1.0)
+        interleave_a(0, on_vector)
+        logc_banks = [spread(logc_cols, g, "corr%d" % g) for g in range(2)]
+        rel_banks = [spread(rel_cols, g, "y") for g in range(2)]
+        interleave_a(1, on_vector)
+        spread_out(neg_logc, 0, logc_banks[0], -1.0)
         x_square_on_vector(0)
         quantise_a(0)
         x_quantise(0)
-        spread_out(neg_logc, 1, spread1, -1.0)
-        interleave_a(2, on_s)
-        interleave_a(3, on_v)
+        interleave_a(2, on_scalar)
+        spread_out(neg_logc, 1, logc_banks[1], -1.0)
+        interleave_a(3, on_vector)
         logits(0, 0)
         x_transpose(1)
         logits(1, 0)
+        spread_out(rel_all, 0, rel_banks[0], 1.0)
         x_copy(1)
         quantise_a(1)
         add_logc(0, 0)
-        x_square(1)
+        x_square_on_scalar(1)
         logits(0, 1)
         x_transpose(2)
         add_logc(1, 0)
         logits(1, 1)
+        spread_out(rel_all, 1, rel_banks[1], 1.0)
         x_copy(2)
         add_logc(0, 1)
         x_quantise(1)
-        x_square(2)
-        spread_out(rel_all, 0, rel0, 1.0)
-        spread_out(rel_all, 1, rel1, 1.0)
+        nc.scalar.copy(out=unit32[:], in_=unit_cols[:])
+        for t in range(PACK):
+            nc.scalar.activation(out=unit_diag[:, t, :], in_=ident16[:], func=ACT.Copy, scale=unit32[:, t : t + 1])
 
-        LAST_WEIGHED = -1
-        SQUARE_ON_VECTOR = (4, 6, 7)
-        ROUND_ON_VECTOR = ()
-        x_step = {1: 3, 2: 4, 4: 5, 7: 6, 9: 7}
+        def step_of_turn(q):
+            return q - 2 if q < FIRST_PAIR_SQUARED_ON_VECTOR else 2 * q - 5
 
-        def pair_ok(first):
-            return 0 <= first < PAIRED
-
-        def finish_rows(i):
-            if i <= LAST_WEIGHED:
-                scale_rows(i)
-            else:
-                normalise(i)
-
-        def has(i):
-            return 0 <= i < TILES
+        turned_in_step = {step_of_turn(q): q for q in range(3, PAIRS)}
+        squared_on_scalar_in_step = {2 * q - 5: q for q in range(3, FIRST_PAIR_SQUARED_ON_VECTOR)}
+        squared_on_vector_in_step = {2 * q - 3: q for q in range(FIRST_PAIR_SQUARED_ON_VECTOR, PAIRS)}
 
         for s in range(1, TILES):
-            odd = s % 2 == 1
-            late = s >= 99
-            q_x = x_step.get(s)
-            if 0 <= s - 2 <= LAST_WEIGHED:
-                weigh(s - 2)
-            if has(s - 3):
-                h_transpose(s - 3)
-            if not odd and has(s - 6):
-                y_transpose([s - 6, s - 5])
+            even = s % 2 == 0
             if s >= 2:
-                logits(s, 1)
-            if q_x is not None:
-                x_transpose(q_x)
-            if has(s - 1):
-                row_max(s - 1)
-            if has(s - 4):
-                c_copy(s - 4, 0, late)
+                weigh(s - 2)
+            if s >= 5:
+                y_round(s - 5, on_scalar, "y")
+            if s >= 3:
+                h_transpose(s - 3)
+            if even and s >= 6:
+                y_transpose([s - 6, s - 5], "xy_turned")
+            if s in turned_in_step:
+                x_transpose(turned_in_step[s])
+            row_max(s - 1)
+            if s >= 4:
+                add_offset_on_scalar(s - 4)
                 y_sum(s - 4)
-            if has(s - 3):
-                h_copy(s - 3, on_s)
-            if has(s - 1):
-                exponent(s - 1)
-            if has(s - 3):
-                y_scaled(s - 3)
-            if has(s):
-                if s >= 2:
-                    add_logc(s, 0)
-                add_logc(s, 1)
-            if has(s + 1):
-                logits(s + 1, 0)
-            else:
-                y_scaled(s - 1, "z")
-                y_scaled(s, "z")
-            if has(s - 2):
-                invert(s - 2)
+            if s >= 3:
+                h_copy(s - 3)
+            exponent(s - 1)
             if s == 1:
-                nc.scalar.copy(out=unit32[:], in_=unit_cols[:])
-                for j in range(4):
-                    nc.scalar.activation(out=unit_diag[:, j, :], in_=ident16[:], func=ACT.Copy, scale=unit32[:, j : j + 1])
-            if has(s - 3):
+                x_square_on_scalar(2)
+            if s >= 3:
+                y_scaled(s - 3, "y")
+            if s >= 2:
+                add_logc(s, 0)
+            add_logc(s, 1)
+            if s + 1 < TILES:
+                logits(s + 1, 0)
+            if s >= 2:
+                invert(s - 2)
+            if s >= 3:
                 h_quantise(s - 3)
                 correction(s - 3)
-            if has(s - 4):
-                y_copy(s - 4, on_s)
-                if s - 4 not in ROUND_ON_VECTOR:
-                    y_round(s - 4, on_s, "y")
-            if not odd and has(s - 6):
-                yt_copy([s - 6, s - 5], on_v if late else on_s)
-            if odd and has(s - 7):
+            if s + 1 < TILES:
+                logits(s + 1, 1)
+            if s >= 4:
+                y_store(s - 4)
+            if even and s >= 6:
+                y_turned_copy([s - 6, s - 5], on_scalar)
+            if not even and s >= 7:
                 y_quantise((s - 7) // 2)
-            if not odd and s // 2 + 1 < PAIRS:
+            if even and s // 2 + 1 < PAIRS:
                 x_quantise(s // 2 + 1)
-            if odd and (s + 3) // 2 in SQUARE_ON_VECTOR:
-                x_square_on_vector((s + 3) // 2)
-            if q_x is not None:
-                x_copy(q_x)
-                if q_x not in SQUARE_ON_VECTOR:
-                    x_square(q_x)
-            if s - 4 in ROUND_ON_VECTOR:
-                y_round(s - 4, on_v, "y32")
-            if has(s - 2):
-                finish_rows(s - 2)
+            if s in squared_on_vector_in_step:
+                x_square_on_vector(squared_on_vector_in_step[s])
+            if s in turned_in_step:
+                x_copy(turned_in_step[s])
+            if s in squared_on_scalar_in_step:
+                x_square_on_scalar(squared_on_scalar_in_step[s])
+            if s >= 2:
+                normalise(s - 2, GPSIMD_COLS)
 
-        a, b, c, d = TILES - 4, TILES - 3, TILES - 2, TILES - 1
+        a, b, c, d = range(TILES - 4, TILES)
+        y_round(a - 1, on_scalar, "y")
         h_transpose(b)
-        y_transpose([a - 2, a - 1])
+        y_transpose([a - 2, a - 1], "xy_turned")
         row_max(d)
-        c_copy(a, 0)
+        h_copy(b)
         exponent(d)
-        h_copy(b, on_s)
         invert(c)
+        add_offset_on_vector(a)
+        y_scaled(b, "y")
+        y_scaled(c, "logits")
         y_sum(a)
-        y_scaled(b)
-        finish_rows(c)
+        normalise(c, 0)
         h_transpose(c)
+        y_scaled(d, "logits")
         invert(d)
         h_quantise(b)
         correction(b)
-        h_copy(c, on_s)
-        normalise(d)
-        y_copy(a, on_s)
+        y_turned_copy([a - 2, a - 1], on_scalar)
+        h_copy(c)
+        normalise(d, 0)
+        y_store(a)
         h_transpose(d)
         h_quantise(c)
         correction(c)
-        h_copy(d, on_s)
-        c_copy(b, 0, True)
+        h_copy(d)
+        add_offset_on_vector(b)
         y_sum(b)
-        yt_copy([a - 2, a - 1], on_s)
+        y_round(a, on_vector, "y32")
         h_quantise(d)
-        c_copy(c, 0, True)
+        add_offset_on_vector(c)
         correction(d)
-        y_copy(b, on_s)
+        y_round(b, on_scalar, "y")
+        y_store(b)
         y_sum(c)
-        y_round(a, on_v, "y32")
+        y_transpose([a, b], "xy_turned")
         y_quantise(a // 2 - 1)
-        c_copy(d, 0, True)
-        y_round(c, on_s, "y")
+        y_round(c, on_scalar, "y")
+        add_offset_on_vector(d)
         y_sum(d)
-        y_round(b, on_v, "y32")
-        y_transpose([c], "ht")
-        y_transpose([a, b])
-        y_round(d, on_s, "y")
-        yt_copy([c], on_v)
-        y_transpose([d], "c0")
-        y_copy(c, on_s)
-        yt_copy([a, b], on_v)
-        y_copy(d, on_s)
-        yt_copy([d], on_v)
+        y_transpose([c], "h_turned")
+        y_turned_copy([a, b], on_vector)
+        y_round(d, on_scalar, "y")
+        y_transpose([d], "corr0")
+        y_turned_copy([c], on_vector)
         y_quantise(a // 2)
+        y_turned_copy([d], on_vector)
+        y_store(c)
+        y_store(d)
         y_quantise(c // 2)
-        store_scales(0, T, [nc.scalar, nc.sync])
+        for quad, queue in enumerate((nc.scalar, nc.sync, nc.scalar, nc.sync)):
+            queue.dma_start(
+                out=out_2[0, 4 * quad : 4 * quad + 4, :].bitcast(I32),
+                in_=y_scales[32 * quad : 32 * quad + 4, :].bitcast(I32),
+            )

from contextlib import ExitStack

import concourse.mybir as mybir
from concourse.masks import make_identity

T, D, C = 2048, 512, 1024
FLOPS = 2 * T * D * C * 3

F32 = mybir.dt.float32
BF16 = mybir.dt.bfloat16
I32 = mybir.dt.int32
U32 = mybir.dt.uint32
U8 = mybir.dt.uint8
FP8X4 = mybir.dt.float8_e4m3fn_x4
FP4X4 = mybir.dt.float4_e2m1fn_x4
ALU = mybir.AluOpType
ACT = mybir.ActivationFunctionType

P = 128
PACK = 4
BANK = 512
TILES = T // P
PAIRS = TILES // 2
A_PART = 256
GPSIMD_COLS = 704
FIRST_PAIR_SQUARED_ON_VECTOR = 5


def tile_gmm_posterior_frame_correction_k6_kernel(
    tc, frames, lin, quad_words, quad_scales, logc, rel, corr_words, corr_scales, unit, offset, out_0, out_1, out_2
):
    nc = tc.nc
    with ExitStack() as ctx:
        keep = ctx.enter_context(tc.tile_pool(name="keep", bufs=1))
        work = ctx.enter_context(tc.tile_pool(name="work", bufs=2))
        psum = ctx.enter_context(tc.psum_pool(name="psum", bufs=1))
        ctx.enter_context(tc.manual_schedule())

        def kept(name, shape, dtype):
            return keep.tile(shape, dtype, name=name, align_bytes=64)

        def flowing(name, shape, dtype, bufs):
            return work.tile(shape, dtype, name=name, tag=name, bufs=bufs, align_bytes=64)

        banks = {"logits": 2, "h_turned": 1, "corr0": 1, "corr1": 1, "y": 2, "xy_turned": 1}

        def bank(tag):
            return psum.tile([P, BANK], F32, name=tag, tag=tag, bufs=banks[tag])

        ident32 = kept("ident32", [P, P], F32)
        ident16 = kept("ident16", [P, P], BF16)
        b_words = kept("b_words", [P, 2 * C], U8)
        b_scales = kept("b_scales", [P, C], U8)
        r_words = kept("r_words", [P, 2, D], U32)
        r_scales = kept("r_scales", [P, 2, D], U8)
        y_scales = kept("y_scales", [P, T], U8)
        logc_cols = kept("logc_cols", [P, 2, PACK], BF16)
        rel_cols = kept("rel_cols", [P, 2, PACK], BF16)
        unit_cols = kept("unit_cols", [P, PACK], BF16)
        unit32 = kept("unit32", [P, PACK], F32)
        offset_cols = kept("offset_cols", [P, 4, 2], BF16)
        neg_logc = kept("neg_logc", [P, C], F32)
        rel_all = kept("rel_all", [P, C], F32)
        unit_diag = kept("unit_diag", [P, PACK, P], BF16)
        table_in = kept("table_in", [P, 1], F32)
        table_out = kept("table_out", [P, 1], F32)
        x_raw = [kept("x_raw%d" % q, [P, 2 * D], BF16) for q in range(PAIRS)]
        x_t = [kept("x_t%d" % q, [P, 4 * D], BF16) for q in range(PAIRS)]
        x_codes = [kept("x_codes%d" % q, [P, D], U32) for q in range(PAIRS)]
        x_scales = [kept("x_scales%d" % q, [P, D], U8) for q in range(PAIRS)]
        a_raw = [kept("a_raw%d" % n, [P, PACK, A_PART], BF16) for n in range(C // A_PART)]
        a_grouped = [kept("a_grouped%d" % g, [P, BANK, PACK], BF16) for g in range(2)]
        a_codes = [kept("a_codes%d" % g, [P, BANK], U32) for g in range(2)]
        a_scales = [kept("a_scales%d" % g, [P, BANK], U8) for g in range(2)]
        live = {}

        on_scalar = nc.scalar.copy
        on_vector = nc.vector.tensor_copy

        def sorted_view(ap):
            return ap.rearrange("p (u m e) -> p u m e", u=2, e=2)

        def natural_as_sorted(ap):
            return ap.rearrange("p (m u e) -> p u m e", u=2, e=2)

        def quantise(codes, scales, values):
            nc.vector.quantize_mx(out=codes.bitcast(FP8X4), scales=scales, in_=values)


        def load_x(q):
            rows = frames[2 * P * q : 2 * P * (q + 1), :]
            nc.sync.dma_start(
                out=x_raw[q][:].rearrange("p (h d) -> p h d", h=2), in_=rows.rearrange("(h p) d -> p h d", h=2)
            )

        def load_a(n):
            rows = lin.rearrange("(p t) c -> p t c", t=PACK)
            nc.sync.dma_start(out=a_raw[n][:], in_=rows[:, :, A_PART * n : A_PART * (n + 1)])

        def load_cols(cols, vec):
            nc.sync.dma_start(out=cols[:], in_=vec.rearrange("(g m t) -> m g t", g=2, t=PACK))

        def interleave_a(n, copy):
            g, half = divmod(n, 2)
            copy(
                out=a_grouped[g][:, A_PART * half : A_PART * (half + 1), :].rearrange("p (c i) t -> p c t i", i=4),
                in_=a_raw[n][:].rearrange("p t (c i) -> p c t i", i=4),
            )

        def quantise_a(g):
            quantise(a_codes[g][:], a_scales[g][:], a_grouped[g][:].rearrange("p c t -> p (c t)"))

        def spread(cols, g, tag):
            ps = bank(tag)
            for t in range(PACK):
                nc.tensor.matmul(
                    out=sorted_view(ps[:])[:, t // 2, :, t % 2], lhsT=cols[:, g, t : t + 1].to_broadcast([P, P]),
                    rhs=ident16[:], start=True, stop=True,
                )
            return ps

        def spread_out(dst, g, ps, sign):
            nc.scalar.activation(out=dst[:, BANK * g : BANK * (g + 1)], in_=ps[:], func=ACT.Copy, scale=sign)


        def x_transpose(q):
            ps = bank("xy_turned")
            words = x_raw[q][:].bitcast(F32).rearrange("p (h m u) -> p h u m", h=2, u=2)
            for h in range(2):
                for u in range(2):
                    slot = 2 * h + u
                    nc.tensor.transpose(ps[:, P * slot : P * (slot + 1)], words[:, h, u, :], ident32[:])
            live["x_turned", q] = ps

        def x_copy(q):
            nc.scalar.copy(
                out=x_t[q][:, 0 : 2 * D].bitcast(F32).rearrange("p (h f u) -> p h f u", h=2, u=2),
                in_=live.pop(("x_turned", q))[:].rearrange("p (h u f) -> p h f u", h=2, u=2),
            )

        def x_square_on_scalar(q):
            nc.scalar.activation(out=x_t[q][:, 2 * D : 4 * D], in_=x_t[q][:, 0 : 2 * D], func=ACT.Square)

        def x_square_on_vector(q):
            x = x_t[q][:, 0 : 2 * D]
            nc.vector.tensor_tensor(out=x_t[q][:, 2 * D : 4 * D], in0=x, in1=x, op=ALU.mult)

        def x_quantise(q):
            quantise(x_codes[q][:], x_scales[q][:], x_t[q][:])


        def logits(i, g):
            q, h = divmod(i, 2)
            ps = bank("logits")
            plain = slice(P * h, P * (h + 1))
            squared = slice(2 * P + P * h, 2 * P + P * (h + 1))
            nc.tensor.matmul_mx(
                out=ps[:], lhsT=x_codes[q][:, plain].bitcast(FP8X4), lhsT_scale=x_scales[q][:, plain],
                rhs=a_codes[g][:].bitcast(FP8X4), rhs_scale=a_scales[g][:], start=True, stop=False,
            )
            nc.tensor.matmul_mx(
                out=ps[:], lhsT=x_codes[q][:, squared].bitcast(FP8X4), lhsT_scale=x_scales[q][:, squared],
                rhs=b_words[:, 2 * BANK * g : 2 * BANK * (g + 1)].bitcast(FP4X4),
                rhs_scale=b_scales[:, BANK * g : BANK * (g + 1)], start=False, stop=True,
            )
            live["z", i, g] = ps

        def add_logc(i, g):
            if g == 0:
                live["neg_z", i] = flowing("neg_z", [P, C], F32, 3)
            cols = slice(BANK * g, BANK * (g + 1))
            nc.vector.tensor_tensor(
                out=sorted_view(live["neg_z", i][:, cols]), in0=sorted_view(neg_logc[:, cols]),
                in1=natural_as_sorted(live.pop(("z", i, g))[:]), op=ALU.subtract,
            )

        def row_max(i):
            neg_max = flowing("neg_max", [P, 1], F32, 3)
            nc.vector.tensor_reduce(out=neg_max[:], in_=live["neg_z", i][:], axis=mybir.AxisListType.X, op=ALU.min)
            live["neg_max", i] = neg_max

        def exponent(i):
            exps = flowing("exps", [P, C], F32, 3)
            total = flowing("total", [P, 1], F32, 3)
            nc.scalar.activation(
                out=exps[:], in_=live.pop(("neg_z", i))[:], func=ACT.Exp, bias=live.pop(("neg_max", i))[:], scale=-1.0,
                accum_out=total[:],
            )
            live["exps", i] = exps
            live["total", i] = total

        def invert(i):
            inv = flowing("inv", [P, 1], F32, 3)
            nc.vector.reciprocal(out=inv[:], in_=live.pop(("total", i))[:])
            live["inv", i] = inv

        def weigh(i):
            weighted = flowing("weighted", [P, GPSIMD_COLS], F32, 1)
            nc.gpsimd.tensor_tensor(
                out=weighted[:], in0=live["exps", i][:, 0:GPSIMD_COLS], in1=rel_all[:, 0:GPSIMD_COLS], op=ALU.mult
            )
            live["weighted", i] = weighted

        def normalise(i, weighed):
            h16 = flowing("h16", [P, C], BF16, 3)
            inv = live.pop(("inv", i))
            nc.vector.scalar_tensor_tensor(
                out=h16[:, weighed:C], in0=live.pop(("exps", i))[:, weighed:C], scalar=inv[:], in1=rel_all[:, weighed:C],
                op0=ALU.mult, op1=ALU.mult,
            )
            if weighed:
                nc.vector.tensor_scalar(
                    out=h16[:, 0:weighed], in0=live.pop(("weighted", i))[:], scalar1=inv[:], scalar2=None, op0=ALU.mult
                )
            live["h16", i] = h16


        def h_transpose(i):
            ps = bank("h_turned")
            words = live.pop(("h16", i))[:].bitcast(F32)
            for slot in range(4):
                cols = slice(P * slot, P * (slot + 1))
                nc.tensor.transpose(ps[:, cols], words[:, cols], ident32[:])
            live["h_turned", i] = ps

        def h_copy(i):
            h_t = flowing("h_t", [P, C], BF16, 3)
            nc.scalar.copy(
                out=h_t[:].bitcast(F32).rearrange("p (g f u) -> p g f u", g=2, u=2),
                in_=live.pop(("h_turned", i))[:].rearrange("p (g u f) -> p g f u", g=2, u=2),
            )
            live["h_t", i] = h_t

        def h_quantise(i):
            codes = flowing("h_codes", [P, 2 * P], U32, 3)
            scales = flowing("h_scales", [P, 2 * P], U8, 3)
            quantise(codes[:], scales[:], live.pop(("h_t", i))[:])
            live["h_mx", i] = (codes, scales)

        def correction(i):
            codes, scales = live.pop(("h_mx", i))
            ps = bank("corr%d" % (i % 2))
            for k in range(4):
                chunk = slice(P * k, P * (k + 1))
                for g in range(2):
                    half = slice(P * g, P * (g + 1))
                    nc.tensor.matmul_mx(
                        out=ps[:, chunk], lhsT=r_words[:, g, chunk].bitcast(FP8X4), lhsT_scale=r_scales[:, g, chunk],
                        rhs=codes[:, half].bitcast(FP8X4), rhs_scale=scales[:, half], start=(g == 0), stop=(g == 1),
                    )
            live["corr", i] = ps

        def add_offset_on_scalar(i):
            c_t = flowing("c_t", [P, 4, P], F32, 4)
            ps = live.pop(("corr", i))
            for k in range(4):
                nc.scalar.activation(
                    out=c_t[:, k, :], in_=ps[:, P * k : P * (k + 1)], func=ACT.Identity, bias=offset_cols[:, k, 0:1]
                )
            live["c_t", i] = c_t

        def add_offset_on_vector(i):
            c_t = flowing("c_t", [P, 4, P], F32, 4)
            nc.vector.tensor_tensor(
                out=c_t[:], in0=live.pop(("corr", i))[:].rearrange("p (k f) -> p k f", k=4),
                in1=offset_cols[:, :, 0:1].to_broadcast([P, 4, P]), op=ALU.add,
            )
            live["c_t", i] = c_t

        def y_scaled(i, tag):
            q, h = divmod(i, 2)
            ps = bank(tag)
            x_slots = x_t[q][:, 0 : 2 * D].rearrange("p (h f t) -> p h t f", h=2, t=PACK)
            y_slots = ps[:].rearrange("f (m t) -> f t m", t=PACK)
            for t in range(PACK):
                nc.tensor.matmul(
                    out=y_slots[:, t, :], lhsT=x_slots[:, h, t, :], rhs=unit_diag[:, t, :], start=(t == 0), stop=False
                )
            live["y", i] = ps

        def y_sum(i):
            c_t = live.pop(("c_t", i))
            for k in range(4):
                nc.tensor.matmul(
                    out=live["y", i][:, P * k : P * (k + 1)], lhsT=c_t[:, k, :], rhs=ident32[:],
                    is_transpose=True, start=False, stop=(k == 3),
                )

        def y_store(i):
            y32 = flowing("y32", [P, D], F32, 6)
            nc.scalar.copy(out=y32[:], in_=live["y", i][:])
            nc.sync.dma_start(out=out_0[P * i : P * (i + 1), :], in_=y32[:])
            live["y32", i] = y32

        def y_round(i, copy, source):
            y16 = flowing("y16", [P, D], BF16, 6)
            copy(out=sorted_view(y16[:]), in_=natural_as_sorted(live[source, i][:]))
            live["y16", i] = y16

        def y_transpose(tiles, tag):
            ps = bank(tag)
            for n, i in enumerate(tiles):
                words = live.pop(("y16", i))[:].bitcast(F32)
                for u in range(2):
                    slot = 2 * n + u
                    nc.tensor.transpose(ps[:, P * slot : P * (slot + 1)], words[:, P * u : P * (u + 1)], ident32[:])
            live["y_turned", tiles[0]] = ps

        def y_turned_copy(tiles, copy):
            q, h = divmod(tiles[0], 2)
            n = len(tiles)
            if h == 0:
                live["y_t", q] = flowing("y_t", [P, 2 * D], BF16, 3)
            copy(
                out=live["y_t", q][:, D * h : D * (h + n)].bitcast(F32).rearrange("p (h f u) -> p h f u", h=n, u=2),
                in_=live.pop(("y_turned", tiles[0]))[:, 0 : 2 * P * n].rearrange("p (h u f) -> p h f u", h=n, u=2),
            )

        def y_quantise(q):
            codes = flowing("y_codes", [P, 2 * P], U32, 4)
            pair_frames = slice(2 * P * q, 2 * P * (q + 1))
            quantise(codes[:], y_scales[:, pair_frames], live.pop(("y_t", q))[:])
            words = out_1[0].rearrange("p m t -> p (m t)").bitcast(I32)
            nc.sync.dma_start(out=words[:, pair_frames], in_=codes[:].bitcast(I32))

        nc.vector.memset(table_in[:], 0.0)
        nc.vector.memset(b_scales[:].bitcast(I32), 0)
        nc.vector.memset(r_scales[:].rearrange("p g n -> p (g n)").bitcast(I32), 0)
        nc.scalar.activation(out=table_out[:], in_=table_in[:], func=ACT.Exp)
        make_identity(nc, ident32[:])
        make_identity(nc, ident16[:])

        load_x(0)
        load_cols(logc_cols, logc)
        load_cols(rel_cols, rel)
        load_a(0)
        load_a(1)
        nc.sync.dma_start(out=b_words[:].bitcast(I32), in_=quad_words[0].bitcast(I32))
        for quad in range(4):
            nc.sync.dma_start(
                out=b_scales[32 * quad : 32 * quad + 4, :].bitcast(I32),
                in_=quad_scales[0, 4 * quad : 4 * quad + 4, :].bitcast(I32),
            )
        load_a(2)
        load_a(3)
        load_x(1)
        load_x(2)
        nc.sync.dma_start(out=unit_cols[:], in_=unit.rearrange("(m t) -> m t", t=PACK))
        load_x(3)
        load_x(4)
        nc.sync.dma_start(out=r_words[:].bitcast(I32), in_=corr_words.rearrange("g p n t -> p g (n t)").bitcast(I32))
        for quad in range(4):
            nc.sync.dma_start(
                out=r_scales[32 * quad : 32 * quad + 4, :, :].bitcast(I32),
                in_=corr_scales[:, 4 * quad : 4 * quad + 4, :].rearrange("g r n -> r g n").bitcast(I32),
            )
        with nc.allow_non_contiguous_dma(reason="one offset a partition for each chunk of 128 channels"):
            nc.sync.dma_start(out=offset_cols[:, :, 0], in_=offset.rearrange("(k p) -> p k", p=P))
        for q in range(5, PAIRS):
            load_x(q)

        x_transpose(0)
        x_copy(0)
        interleave_a(0, on_vector)
        logc_banks = [spread(logc_cols, g, "corr%d" % g) for g in range(2)]
        rel_banks = [spread(rel_cols, g, "y") for g in range(2)]
        interleave_a(1, on_vector)
        spread_out(neg_logc, 0, logc_banks[0], -1.0)
        x_square_on_vector(0)
        quantise_a(0)
        x_quantise(0)
        interleave_a(2, on_scalar)
        spread_out(neg_logc, 1, logc_banks[1], -1.0)
        interleave_a(3, on_vector)
        logits(0, 0)
        x_transpose(1)
        logits(1, 0)
        spread_out(rel_all, 0, rel_banks[0], 1.0)
        x_copy(1)
        quantise_a(1)
        add_logc(0, 0)
        x_square_on_scalar(1)
        logits(0, 1)
        x_transpose(2)
        add_logc(1, 0)
        logits(1, 1)
        spread_out(rel_all, 1, rel_banks[1], 1.0)
        x_copy(2)
        add_logc(0, 1)
        x_quantise(1)
        nc.scalar.copy(out=unit32[:], in_=unit_cols[:])
        for t in range(PACK):
            nc.scalar.activation(out=unit_diag[:, t, :], in_=ident16[:], func=ACT.Copy, scale=unit32[:, t : t + 1])

        def step_of_turn(q):
            return q - 2 if q < FIRST_PAIR_SQUARED_ON_VECTOR else 2 * q - 5

        turned_in_step = {step_of_turn(q): q for q in range(3, PAIRS)}
        squared_on_scalar_in_step = {2 * q - 5: q for q in range(3, FIRST_PAIR_SQUARED_ON_VECTOR)}
        squared_on_vector_in_step = {2 * q - 3: q for q in range(FIRST_PAIR_SQUARED_ON_VECTOR, PAIRS)}

        for s in range(1, TILES):
            even = s % 2 == 0
            if s >= 2:
                weigh(s - 2)
            if s >= 5:
                y_round(s - 5, on_scalar, "y")
            if s >= 3:
                h_transpose(s - 3)
            if even and s >= 6:
                y_transpose([s - 6, s - 5], "xy_turned")
            if s in turned_in_step:
                x_transpose(turned_in_step[s])
            row_max(s - 1)
            if s >= 4:
                add_offset_on_scalar(s - 4)
                y_sum(s - 4)
            if s >= 3:
                h_copy(s - 3)
            exponent(s - 1)
            if s == 1:
                x_square_on_scalar(2)
            if s >= 3:
                y_scaled(s - 3, "y")
            if s >= 2:
                add_logc(s, 0)
            add_logc(s, 1)
            if s + 1 < TILES:
                logits(s + 1, 0)
            if s >= 2:
                invert(s - 2)
            if s >= 3:
                h_quantise(s - 3)
                correction(s - 3)
            if s + 1 < TILES:
                logits(s + 1, 1)
            if s >= 4:
                y_store(s - 4)
            if even and s >= 6:
                y_turned_copy([s - 6, s - 5], on_scalar)
            if not even and s >= 7:
                y_quantise((s - 7) // 2)
            if even and s // 2 + 1 < PAIRS:
                x_quantise(s // 2 + 1)
            if s in squared_on_vector_in_step:
                x_square_on_vector(squared_on_vector_in_step[s])
            if s in turned_in_step:
                x_copy(turned_in_step[s])
            if s in squared_on_scalar_in_step:
                x_square_on_scalar(squared_on_scalar_in_step[s])
            if s >= 2:
                normalise(s - 2, GPSIMD_COLS)

        a, b, c, d = range(TILES - 4, TILES)
        y_round(a - 1, on_scalar, "y")
        h_transpose(b)
        y_transpose([a - 2, a - 1], "xy_turned")
        row_max(d)
        h_copy(b)
        exponent(d)
        invert(c)
        add_offset_on_vector(a)
        y_scaled(b, "y")
        y_scaled(c, "logits")
        y_sum(a)
        normalise(c, 0)
        h_transpose(c)
        y_scaled(d, "logits")
        invert(d)
        h_quantise(b)
        correction(b)
        y_turned_copy([a - 2, a - 1], on_scalar)
        h_copy(c)
        normalise(d, 0)
        y_store(a)
        h_transpose(d)
        h_quantise(c)
        correction(c)
        h_copy(d)
        add_offset_on_vector(b)
        y_sum(b)
        y_round(a, on_vector, "y32")
        h_quantise(d)
        add_offset_on_vector(c)
        correction(d)
        y_round(b, on_scalar, "y")
        y_store(b)
        y_sum(c)
        y_transpose([a, b], "xy_turned")
        y_quantise(a // 2 - 1)
        y_round(c, on_scalar, "y")
        add_offset_on_vector(d)
        y_sum(d)
        y_transpose([c], "h_turned")
        y_turned_copy([a, b], on_vector)
        y_round(d, on_scalar, "y")
        y_transpose([d], "corr0")
        y_turned_copy([c], on_vector)
        y_quantise(a // 2)
        y_turned_copy([d], on_vector)
        y_store(c)
        y_store(d)
        y_quantise(c // 2)
        for quad, queue in enumerate((nc.scalar, nc.sync, nc.scalar, nc.sync)):
            queue.dma_start(
                out=out_2[0, 4 * quad : 4 * quad + 4, :].bitcast(I32),
                in_=y_scales[32 * quad : 32 * quad + 4, :].bitcast(I32),
            )
